import numpy as np
import ml_dtypes


def mxq(x, axis, fmt="e4m3"):
    dtype, down = {"e4m3": (ml_dtypes.float8_e4m3fn, 7), "e5m2": (ml_dtypes.float8_e5m2, 14)}[fmt]
    v = np.moveaxis(np.asarray(x, np.float32).astype(ml_dtypes.bfloat16).astype(np.float64), axis, -1)
    blocks = v.reshape(v.shape[:-1] + (-1, 32))
    amax = np.abs(blocks).max(-1, keepdims=True)
    byte = np.maximum(np.where(amax > 0, np.frexp(amax)[1] - 1 + 127, 0) - down, 1)
    scale = np.exp2(byte - 127.0)
    codes = (blocks / scale).astype(np.float32).astype(dtype).astype(np.float64)
    return np.moveaxis((codes * scale).reshape(v.shape), -1, axis)


WIDE = False


def mx_kscale(k):
    if not WIDE:
        return np.ones(k)
    levels = np.array([10, -10, 5, -5, 0])
    if k % 512:
        return np.exp2(np.random.permutation(np.resize(levels, k // 32))).repeat(32)
    a = np.empty((k // 512, 16))
    for p in range(k // 512):
        a[p, :8] = np.random.permutation(np.resize(levels, 8))
        for g in range(8):
            far = levels[np.abs(levels - a[p, g]) >= 10]
            a[p, g + 8] = far[np.random.randint(len(far))]
    return np.exp2(a.ravel()).repeat(32)


BF16 = ml_dtypes.bfloat16


def bf(x):
    return np.asarray(x, np.float32).astype(BF16)


def f64(x):
    return np.asarray(x).astype(np.float64)

def planes(Y):
    n, m = Y.shape
    b = f64(bf(Y)).reshape(n // 32, 32, m)
    amax = np.abs(b).max(1)
    byte = np.clip(np.where(amax > 0, np.frexp(amax)[1] - 1 + 127 - 7, 1), 1, 254)
    codes = (b * np.exp2(127.0 - byte)[:, None, :]).reshape(n, m).astype(np.float32).astype(ml_dtypes.float8_e4m3fn).view(np.uint8)
    words = codes.reshape(n // 512, 128, 4, m).transpose(0, 1, 3, 2)
    return np.ascontiguousarray(words), np.ascontiguousarray(byte.astype(np.uint8).reshape(n // 512, 16, m))


M, N, B = 1024, 2048, 768


def setup_inputs():
    s = mx_kscale(N)
    t = mx_kscale(M)
    spread = np.exp(0.7 * np.random.randn(N))
    sense = np.random.randn(M, N) / np.sqrt(N) * t[:, None] * s[None, :]
    est = 0.6 * np.random.exponential(size=(N, B)) ** 1.3 / s[:, None]
    meas = 1.2 * np.random.randn(M, B) * t[:, None]
    weight = np.exp(0.3 * np.random.randn(M)) / t ** 2
    gain = spread * s
    step = 0.4 * spread * np.exp(0.2 * np.random.randn(N)) / s
    return {"sense": bf(sense), "est": bf(est), "meas": bf(meas),
            "weight": bf(weight), "gain": bf(gain), "step": bf(step)}


def reference(sense, est, meas, weight, gain, step):
    a, x, obs = f64(sense), f64(est), f64(meas)
    w, c, h = f64(weight), f64(gain), f64(step)
    pred = mxq(a, 1, "e4m3") @ mxq(x, 0, "e4m3")
    r = w[:, None] * (obs - pred)
    back = mxq(a, 0, "e4m3").T @ mxq(r, 0, "e4m3")
    u = c[:, None] * x + h[:, None] * back
    y = u / (1.0 + np.exp(-u))
    Y = y.reshape(N, B)
    words, scales = planes(Y)
    return y, words, scales

@@ -1,0 +1,407 @@
+from contextlib import ExitStack
+
+import concourse.mybir as mybir
+from concourse.masks import make_identity
+
+M, N, B = 1024, 2048, 768
+FLOPS = 2 * 2 * M * N * B
+
+F32 = mybir.dt.float32
+BF16 = mybir.dt.bfloat16
+U32 = mybir.dt.uint32
+I32 = mybir.dt.int32
+U8 = mybir.dt.uint8
+FP8X4 = mybir.dt.float8_e4m3fn_x4
+ACT = mybir.ActivationFunctionType
+ALU = mybir.AluOpType
+
+P = 128
+PACK = 4
+GROUP = P * PACK
+M_GROUPS = M // GROUP
+N_GROUPS = N // GROUP
+BANK = 512
+WIDE, NARROW = 0, 1
+COL0 = (0, 512)
+WIDTH = (512, 256)
+
+
+def tile_sensing_residual_shrink_step_h3_kernel(
+    tc, sense, est, meas, weight, gain, step, out_0, out_1, out_2
+):
+    nc = tc.nc
+    with ExitStack() as ctx:
+        keep = ctx.enter_context(tc.tile_pool(name="keep", bufs=1))
+        ring = ctx.enter_context(tc.tile_pool(name="ring", bufs=2))
+        psum = ctx.enter_context(tc.psum_pool(name="psum", bufs=1))
+        ctx.enter_context(tc.manual_schedule())
+
+        def cols(c):
+            return slice(COL0[c], COL0[c] + WIDTH[c])
+
+        def rows4(dram, g):
+            return dram[g * GROUP : (g + 1) * GROUP, :].rearrange("(p t) w -> p t w", t=PACK)
+
+        def bank(i):
+            return psum.tile([P, BANK], F32, name="bank%d" % i, tag="bank%d" % i)
+
+        def operand(name, width):
+            codes = keep.tile([P, width], U32, name=name + "_codes", align_bytes=64)
+            scales = keep.tile([P, width], U8, name=name + "_scales", align_bytes=64)
+            return codes, scales
+
+        def quantize(codes, scales, staged):
+            nc.vector.quantize_mx(out=codes.bitcast(FP8X4), scales=scales, in_=staged)
+
+        def packed_view(staged):
+            return staged.rearrange("p (c i t) -> p c t i", i=4, t=PACK)
+
+        def slots_view(slots):
+            return slots.rearrange("p t (c i) -> p c t i", i=4)
+
+        def stage_v(width):
+            staged = ring.tile([P, PACK * width], BF16, name="stage_v", tag="stage_v", bufs=3, align_bytes=64)
+            return staged
+
+        def stage_s(width):
+            staged = ring.tile([P, PACK * width], BF16, name="stage_s", tag="stage_s", bufs=3, align_bytes=64)
+            return staged
+
+        gain_bf = keep.tile([P, N_GROUPS, PACK], BF16)
+        weight_bf = keep.tile([P, M_GROUPS, PACK], BF16)
+        step_bf = keep.tile([P, N_GROUPS, PACK], BF16)
+        est_raw, sense_raw, meas_raw = {}, {}, {}
+
+        def load_est(g, c):
+            est_raw[g, c] = keep.tile([P, PACK, WIDTH[c]], BF16, name="est_raw%d_%d" % (g, c))
+            nc.sync.dma_start(out=est_raw[g, c][:], in_=rows4(est, g)[:, :, cols(c)])
+
+        def load_sense(h, g):
+            sense_raw[h, g] = keep.tile([P, PACK, GROUP], BF16, name="sense_raw%d_%d" % (h, g))
+            nc.sync.dma_start(out=sense_raw[h, g][:], in_=rows4(sense, h)[:, :, g * GROUP : (g + 1) * GROUP])
+
+        def load_meas(h, c):
+            meas_raw[h, c] = keep.tile([P, PACK, WIDTH[c]], BF16, name="meas_raw%d_%d" % (h, c))
+            nc.sync.dma_start(out=meas_raw[h, c][:], in_=rows4(meas, h)[:, :, cols(c)])
+
+        def load_vector(tile, vec):
+            nc.scalar.dma_start(out=tile[:], in_=vec.rearrange("(g p t) -> p g t", p=P, t=PACK))
+
+        load_vector(gain_bf, gain)
+        load_vector(weight_bf, weight)
+        load_vector(step_bf, step)
+        for g in range(N_GROUPS):
+            load_est(g, WIDE)
+            load_sense(0, g)
+        load_meas(0, WIDE)
+        for g in range(N_GROUPS):
+            load_sense(1, g)
+        load_meas(1, WIDE)
+        for g in range(N_GROUPS):
+            load_est(g, NARROW)
+        for h in range(M_GROUPS):
+            load_meas(h, NARROW)
+
+        ident = keep.tile([P, P], F32)
+        make_identity(nc, ident[:])
+
+        warm = keep.tile([P, 1], F32)
+        nc.scalar.activation(out=warm[:], in_=ident[:, 0:1], func=ACT.Silu)
+        gain_f = keep.tile([P, N_GROUPS, PACK], F32)
+        weight_f = keep.tile([P, M_GROUPS, PACK], F32)
+        neg_weight_f = keep.tile([P, M_GROUPS, PACK], F32)
+        nc.scalar.copy(out=gain_f[:], in_=gain_bf[:])
+        nc.scalar.copy(out=weight_f[:], in_=weight_bf[:])
+        nc.scalar.activation(out=neg_weight_f[:], in_=weight_bf[:], func=ACT.Copy, scale=-1.0)
+
+        staged = {}
+        est_q, sense_n_q, sense_m_q, resid_q = {}, {}, {}, {}
+        acc, turned, work, wmeas, resid, y_codes = {}, {}, {}, {}, {}, {}
+        y_scales = keep.tile([P, B], U8, align_bytes=64)
+
+        def pack_est(g, c):
+            staged["est", g, c] = stage_v(WIDTH[c])
+            nc.vector.tensor_copy(out=packed_view(staged["est", g, c][:]), in_=slots_view(est_raw[g, c][:]))
+
+        def pack_est_on_scalar(g, c):
+            staged["est", g, c] = stage_s(WIDTH[c])
+            nc.scalar.copy(out=packed_view(staged["est", g, c][:]), in_=slots_view(est_raw[g, c][:]))
+
+        def quant_est(g, c):
+            est_q[g, c] = operand("est%d_%d" % (g, c), WIDTH[c])
+            quantize(est_q[g, c][0][:], est_q[g, c][1][:], staged["est", g, c][:])
+
+        def turn_sense(h, g):
+            first = 4 + 2 * ((h * N_GROUPS + g) % 2)
+            turned[h, g] = [bank(first), bank(first + 1)]
+            for t in range(PACK):
+                words = sense_raw[h, g][:, t, :].bitcast(F32)
+                for u in range(2):
+                    j = 2 * (t % 2) + u
+                    nc.tensor.transpose(turned[h, g][t // 2][:, j * P : (j + 1) * P], words[:, u : 2 * P : 2], ident[:])
+
+        def copy_turned(h, g):
+            staged["turn", h, g] = stage_s(GROUP)
+            dst = staged["turn", h, g][:].bitcast(F32).rearrange("p (t r u) -> p t r u", t=PACK, u=2)
+            for half in range(2):
+                src = turned[h, g][half][:].rearrange("p (t u r) -> p t r u", t=2, u=2)
+                nc.scalar.copy(out=dst[:, 2 * half : 2 * half + 2], in_=src)
+
+        def quant_turned(h, g):
+            sense_n_q[h, g] = operand("sense_n%d_%d" % (h, g), GROUP)
+            quantize(sense_n_q[h, g][0][:], sense_n_q[h, g][1][:], staged["turn", h, g][:])
+
+        def pack_sense(h, g, on_scalar=False):
+            staged["sense", h, g] = stage_s(GROUP) if on_scalar else stage_v(GROUP)
+            dst = staged["sense", h, g][:].rearrange("p (s a i j) -> p a s i j", s=PACK, i=2, j=PACK)
+            src = sense_raw[h, g][:].rearrange("p j (a i s) -> p a s i j", i=2, s=PACK)
+            if on_scalar:
+                nc.scalar.copy(out=dst, in_=src)
+            else:
+                nc.vector.tensor_copy(out=dst, in_=src)
+
+        def quant_sense(h, g):
+            sense_m_q[h, g] = operand("sense_m%d_%d" % (h, g), GROUP)
+            quantize(sense_m_q[h, g][0][:], sense_m_q[h, g][1][:], staged["sense", h, g][:])
+
+        def open_acc(key, c, first_bank, per_bank):
+            banks = [bank(first_bank + i) for i in range(PACK // per_bank)]
+            acc[key] = [
+                banks[t // per_bank][:, (t % per_bank) * WIDTH[c] : (t % per_bank + 1) * WIDTH[c]] for t in range(PACK)
+            ]
+
+        def mx_pass(out, stationary, t, moving, start, stop):
+            nc.tensor.matmul_mx(
+                out=out,
+                lhsT=stationary[0][:, t * P : (t + 1) * P].bitcast(FP8X4),
+                lhsT_scale=stationary[1][:, t * P : (t + 1) * P],
+                rhs=moving[0][:].bitcast(FP8X4),
+                rhs_scale=moving[1][:],
+                start=start,
+                stop=stop,
+            )
+
+        def pred_pass(h, g, c):
+            for t in range(PACK):
+                mx_pass(acc["pred", h, c][t], sense_n_q[h, g], t, est_q[g, c], g == 0, g == N_GROUPS - 1)
+
+        def pred_narrow(h, first_bank):
+            open_acc(("pred", h, NARROW), NARROW, first_bank, 2)
+            for t in range(PACK):
+                for g in range(N_GROUPS):
+                    mx_pass(acc["pred", h, NARROW][t], sense_n_q[h, g], t, est_q[g, NARROW], g == 0, g == N_GROUPS - 1)
+
+        def back(g, c, first_bank):
+            open_acc(("back", g, c), c, first_bank, BANK // WIDTH[c])
+            for t in range(PACK):
+                for h in range(M_GROUPS):
+                    mx_pass(acc["back", g, c][t], sense_m_q[h, g], t, resid_q[h, c], h == 0, h == M_GROUPS - 1)
+
+        def weigh_meas(h, c):
+            wmeas[h, c] = ring.tile([P, PACK, WIDTH[c]], F32, name="wmeas%d" % c, tag="wmeas%d" % c, bufs=1 + c)
+            for t in range(PACK):
+                nc.scalar.activation(
+                    out=wmeas[h, c][:, t, :], in_=meas_raw[h, c][:, t, :], func=ACT.Copy, scale=weight_f[:, h, t : t + 1]
+                )
+
+        def residual(h, c):
+            resid[h, c] = ring.tile([P, PACK, WIDTH[c]], BF16, name="resid", tag="resid")
+            for t in range(PACK):
+                nc.vector.scalar_tensor_tensor(
+                    out=resid[h, c][:, t, :],
+                    in0=acc["pred", h, c][t],
+                    scalar=neg_weight_f[:, h, t : t + 1],
+                    in1=wmeas[h, c][:, t, :],
+                    op0=ALU.mult,
+                    op1=ALU.add,
+                )
+
+        def pack_resid(h, c):
+            staged["resid", h, c] = stage_v(WIDTH[c])
+            nc.vector.tensor_copy(out=packed_view(staged["resid", h, c][:]), in_=slots_view(resid[h, c][:]))
+
+        def quant_resid(h, c):
+            resid_q[h, c] = operand("resid%d_%d" % (h, c), WIDTH[c])
+            quantize(resid_q[h, c][0][:], resid_q[h, c][1][:], staged["resid", h, c][:])
+
+        def gain_est(g, c, lo=0, hi=PACK):
+            if lo == 0:
+                work[g, c] = keep.tile([P, PACK, WIDTH[c]], F32, name="work%d_%d" % (g, c))
+            for t in range(lo, hi):
+                nc.scalar.activation(
+                    out=work[g, c][:, t, :], in_=est_raw[g, c][:, t, :], func=ACT.Copy, scale=gain_f[:, g, t : t + 1]
+                )
+
+        def gain_wide_slots(first, count):
+            for s in range(first, first + count):
+                gain_est(s // PACK, WIDE, s % PACK, s % PACK + 1)
+
+        def stepped(g, c):
+            for t in range(PACK):
+                nc.vector.scalar_tensor_tensor(
+                    out=work[g, c][:, t, :],
+                    in0=acc["back", g, c][t],
+                    scalar=step_bf[:, g, t : t + 1],
+                    in1=work[g, c][:, t, :],
+                    op0=ALU.mult,
+                    op1=ALU.add,
+                )
+
+        def shrink(g, c):
+            staged["y", g, c] = stage_s(WIDTH[c])
+            nc.scalar.activation(out=packed_view(staged["y", g, c][:]), in_=slots_view(work[g, c][:]), func=ACT.Silu)
+            nc.scalar.activation(out=work[g, c][:], in_=work[g, c][:], func=ACT.Silu)
+
+        def shrink_slots(g, c, lo, hi):
+            nc.scalar.activation(out=work[g, c][:, lo:hi, :], in_=work[g, c][:, lo:hi, :], func=ACT.Silu)
+            nc.sync.dma_start(out=rows4(out_0, g)[:, lo:hi, cols(c)], in_=work[g, c][:, lo:hi, :])
+
+        def pack_y(g, c):
+            staged["y", g, c] = stage_v(WIDTH[c])
+            nc.vector.tensor_copy(out=packed_view(staged["y", g, c][:]), in_=slots_view(work[g, c][:]))
+
+        def quant_y(g, c):
+            y_codes[g, c] = ring.tile([P, WIDTH[c]], U32, name="y_codes", tag="y_codes", bufs=4, align_bytes=64)
+            quantize(y_codes[g, c][:], y_scales[PACK * g :, cols(c)], staged["y", g, c][:])
+
+        def store_codes(g, c):
+            words = out_1[g].rearrange("p m t -> p (m t)").bitcast(I32)
+            nc.sync.dma_start(out=words[:, cols(c)], in_=y_codes[g, c][:].bitcast(I32))
+
+        def store_y(g, c):
+            nc.sync.dma_start(out=rows4(out_0, g)[:, :, cols(c)], in_=work[g, c][:])
+
+        last = N_GROUPS - 1
+        open_acc(("pred", 0, WIDE), WIDE, 0, 1)
+        for g in range(N_GROUPS):
+            pack_est(g, WIDE)
+            if g > 0:
+                quant_turned(0, g - 1)
+            quant_est(g, WIDE)
+            gain_wide_slots(3 * g, 3)
+            turn_sense(0, g)
+            if g > 0:
+                pred_pass(0, g - 1, WIDE)
+            copy_turned(0, g)
+            if g == 0:
+                pack_sense(0, 0)
+        quant_sense(0, 0)
+        pack_sense(0, 1)
+        quant_turned(0, last)
+        weigh_meas(0, WIDE)
+        turn_sense(1, 0)
+        pred_pass(0, last, WIDE)
+        copy_turned(1, 0)
+        quant_sense(0, 1)
+        pack_sense(1, 0)
+        turn_sense(1, 1)
+        gain_wide_slots(12, 2)
+        copy_turned(1, 1)
+        quant_turned(1, 0)
+        residual(0, WIDE)
+        open_acc(("pred", 1, WIDE), WIDE, 0, 1)
+        quant_turned(1, 1)
+        turn_sense(1, 2)
+        copy_turned(1, 2)
+        turn_sense(1, 3)
+        copy_turned(1, 3)
+        pred_pass(1, 0, WIDE)
+        pred_pass(1, 1, WIDE)
+        weigh_meas(1, WIDE)
+        quant_sense(1, 0)
+        quant_turned(1, 2)
+        pack_resid(0, WIDE)
+        quant_turned(1, 3)
+        pred_pass(1, 2, WIDE)
+        pred_pass(1, 3, WIDE)
+        quant_resid(0, WIDE)
+        pack_sense(1, 1)
+        gain_wide_slots(14, 2)
+        pack_est_on_scalar(0, NARROW)
+        pack_est_on_scalar(1, NARROW)
+        pack_est_on_scalar(2, NARROW)
+        residual(1, WIDE)
+        quant_sense(1, 1)
+        pack_resid(1, WIDE)
+        quant_est(0, NARROW)
+        quant_resid(1, WIDE)
+        back(0, WIDE, 0)
+        back(1, WIDE, 4)
+        quant_est(1, NARROW)
+        quant_est(2, NARROW)
+        pack_est_on_scalar(3, NARROW)
+        weigh_meas(0, NARROW)
+        weigh_meas(1, NARROW)
+        stepped(0, WIDE)
+        shrink(0, WIDE)
+        store_y(0, WIDE)
+        quant_est(3, NARROW)
+        pred_narrow(0, 0)
+        pred_narrow(1, 2)
+        pack_sense(0, 2)
+        stepped(1, WIDE)
+        shrink(1, WIDE)
+        quant_sense(0, 2)
+        pack_sense(1, 2)
+        quant_y(0, WIDE)
+        store_codes(0, WIDE)
+        store_y(1, WIDE)
+        quant_sense(1, 2)
+        back(2, WIDE, 4)
+        residual(0, NARROW)
+        residual(1, NARROW)
+        pack_resid(0, NARROW)
+        quant_y(1, WIDE)
+        store_codes(1, WIDE)
+        gain_est(0, NARROW)
+        gain_est(1, NARROW)
+        stepped(2, WIDE)
+        shrink(2, WIDE)
+        store_y(2, WIDE)
+        quant_resid(0, NARROW)
+        pack_resid(1, NARROW)
+        pack_sense(0, 3)
+        quant_resid(1, NARROW)
+        back(0, NARROW, 0)
+        back(1, NARROW, 2)
+        quant_sense(0, 3)
+        pack_sense(1, 3)
+        stepped(0, NARROW)
+        quant_sense(1, 3)
+        back(3, WIDE, 4)
+        back(2, NARROW, 0)
+        gain_est(2, NARROW)
+        shrink(0, NARROW)
+        quant_y(2, WIDE)
+        store_codes(2, WIDE)
+        store_y(0, NARROW)
+        stepped(1, NARROW)
+        back(3, NARROW, 2)
+        stepped(3, WIDE)
+        gain_est(3, NARROW)
+        shrink(1, NARROW)
+        quant_y(0, NARROW)
+        store_codes(0, NARROW)
+        stepped(2, NARROW)
+        quant_y(1, NARROW)
+        store_codes(1, NARROW)
+        store_y(1, NARROW)
+        shrink_slots(3, WIDE, 0, 2)
+        shrink_slots(3, WIDE, 2, 4)
+        stepped(3, NARROW)
+        shrink_slots(2, NARROW, 0, 4)
+        shrink_slots(3, NARROW, 0, 4)
+        pack_y(3, WIDE)
+        pack_y(2, NARROW)
+        quant_y(3, WIDE)
+        store_codes(3, WIDE)
+        pack_y(3, NARROW)
+        quant_y(2, NARROW)
+        store_codes(2, NARROW)
+        quant_y(last, NARROW)
+        store_codes(last, NARROW)
+        scale_rows = out_2.bitcast(I32)
+        for q in range(4):
+            nc.scalar.dma_start(
+                out=scale_rows[:, 4 * q : 4 * q + 4, :], in_=y_scales[32 * q : 32 * q + 16, :].bitcast(I32)
+            )

@@ -72,9 +72,11 @@ def tile_sensing_residual_shrink_step_h3_kernel(
         step_bf = keep.tile([P, N_GROUPS, PACK], BF16)
         est_raw, sense_raw, meas_raw = {}, {}, {}
 
-        def load_est(g, c):
-            est_raw[g, c] = keep.tile([P, PACK, WIDTH[c]], BF16, name="est_raw%d_%d" % (g, c))
-            nc.sync.dma_start(out=est_raw[g, c][:], in_=rows4(est, g)[:, :, cols(c)])
+        def load_est(g):
+            whole = keep.tile([P, PACK, B], BF16, name="est_raw%d" % g)
+            nc.sync.dma_start(out=whole[:], in_=rows4(est, g))
+            for c in (WIDE, NARROW):
+                est_raw[g, c] = whole[:, :, cols(c)]
 
         def load_sense(h, g):
             sense_raw[h, g] = keep.tile([P, PACK, GROUP], BF16, name="sense_raw%d_%d" % (h, g))
@@ -85,20 +87,19 @@ def tile_sensing_residual_shrink_step_h3_kernel(
             nc.sync.dma_start(out=meas_raw[h, c][:], in_=rows4(meas, h)[:, :, cols(c)])
 
         def load_vector(tile, vec):
-            nc.scalar.dma_start(out=tile[:], in_=vec.rearrange("(g p t) -> p g t", p=P, t=PACK))
+            nc.sync.dma_start(out=tile[:], in_=vec.rearrange("(g p t) -> p g t", p=P, t=PACK))
 
-        load_vector(gain_bf, gain)
-        load_vector(weight_bf, weight)
-        load_vector(step_bf, step)
         for g in range(N_GROUPS):
-            load_est(g, WIDE)
+            load_est(g)
             load_sense(0, g)
+            if g == 1:
+                load_vector(weight_bf, weight)
+                load_vector(gain_bf, gain)
+                load_vector(step_bf, step)
         load_meas(0, WIDE)
         for g in range(N_GROUPS):
             load_sense(1, g)
         load_meas(1, WIDE)
-        for g in range(N_GROUPS):
-            load_est(g, NARROW)
         for h in range(M_GROUPS):
             load_meas(h, NARROW)
 
@@ -110,9 +111,11 @@ def tile_sensing_residual_shrink_step_h3_kernel(
         gain_f = keep.tile([P, N_GROUPS, PACK], F32)
         weight_f = keep.tile([P, M_GROUPS, PACK], F32)
         neg_weight_f = keep.tile([P, M_GROUPS, PACK], F32)
-        nc.scalar.copy(out=gain_f[:], in_=gain_bf[:])
-        nc.scalar.copy(out=weight_f[:], in_=weight_bf[:])
-        nc.scalar.activation(out=neg_weight_f[:], in_=weight_bf[:], func=ACT.Copy, scale=-1.0)
+
+        def widen_vectors():
+            nc.scalar.copy(out=gain_f[:], in_=gain_bf[:])
+            nc.scalar.copy(out=weight_f[:], in_=weight_bf[:])
+            nc.scalar.activation(out=neg_weight_f[:], in_=weight_bf[:], func=ACT.Copy, scale=-1.0)
 
         staged = {}
         est_q, sense_n_q, sense_m_q, resid_q = {}, {}, {}, {}
@@ -151,14 +154,21 @@ def tile_sensing_residual_shrink_step_h3_kernel(
             sense_n_q[h, g] = operand("sense_n%d_%d" % (h, g), GROUP)
             quantize(sense_n_q[h, g][0][:], sense_n_q[h, g][1][:], staged["turn", h, g][:])
 
-        def pack_sense(h, g, on_scalar=False):
-            staged["sense", h, g] = stage_s(GROUP) if on_scalar else stage_v(GROUP)
-            dst = staged["sense", h, g][:].rearrange("p (s a i j) -> p a s i j", s=PACK, i=2, j=PACK)
-            src = sense_raw[h, g][:].rearrange("p j (a i s) -> p a s i j", i=2, s=PACK)
-            if on_scalar:
-                nc.scalar.copy(out=dst, in_=src)
-            else:
-                nc.vector.tensor_copy(out=dst, in_=src)
+        def sense_views(h, g):
+            dst = staged["sense", h, g][:].rearrange("p (s a i j) -> p a j i s", s=PACK, i=2, j=PACK)
+            src = sense_raw[h, g][:].rearrange("p j (a i s) -> p a j i s", i=2, s=PACK)
+            return dst, src
+
+        def pack_sense(h, g):
+            staged["sense", h, g] = stage_v(GROUP)
+            dst, src = sense_views(h, g)
+            nc.vector.tensor_copy(out=dst, in_=src)
+
+        def pack_sense_half_on_scalar(h, g, half):
+            if half == 0:
+                staged["sense", h, g] = ring.tile([P, PACK * GROUP], BF16, name="stage_h", tag="stage_h", bufs=2, align_bytes=64)
+            dst, src = sense_views(h, g)
+            nc.scalar.copy(out=dst[:, 32 * half : 32 * half + 32], in_=src[:, 32 * half : 32 * half + 32])
 
         def quant_sense(h, g):
             sense_m_q[h, g] = operand("sense_m%d_%d" % (h, g), GROUP)
@@ -198,14 +208,22 @@ def tile_sensing_residual_shrink_step_h3_kernel(
                     mx_pass(acc["back", g, c][t], sense_m_q[h, g], t, resid_q[h, c], h == 0, h == M_GROUPS - 1)
 
         def weigh_meas(h, c):
-            wmeas[h, c] = ring.tile([P, PACK, WIDTH[c]], F32, name="wmeas%d" % c, tag="wmeas%d" % c, bufs=1 + c)
+            if c == WIDE:
+                wmeas[h, c] = ring.tile([P, PACK, WIDTH[c]], F32, name="wmeas", tag="wmeas", bufs=1)
+            elif h == 0:
+                both = ring.tile([P, M_GROUPS, PACK, WIDTH[c]], F32, name="wmeas", tag="wmeas", bufs=1)
+                wmeas[0, c], wmeas[1, c] = both[:, 0], both[:, 1]
             for t in range(PACK):
                 nc.scalar.activation(
                     out=wmeas[h, c][:, t, :], in_=meas_raw[h, c][:, t, :], func=ACT.Copy, scale=weight_f[:, h, t : t + 1]
                 )
 
         def residual(h, c):
-            resid[h, c] = ring.tile([P, PACK, WIDTH[c]], BF16, name="resid", tag="resid")
+            if c == WIDE:
+                resid[h, c] = ring.tile([P, PACK, WIDTH[c]], BF16, name="resid", tag="resid", bufs=1)
+            elif h == 0:
+                both = ring.tile([P, M_GROUPS, PACK, WIDTH[c]], BF16, name="resid", tag="resid", bufs=1)
+                resid[0, c], resid[1, c] = both[:, 0], both[:, 1]
             for t in range(PACK):
                 nc.vector.scalar_tensor_tensor(
                     out=resid[h, c][:, t, :],
@@ -225,7 +243,7 @@ def tile_sensing_residual_shrink_step_h3_kernel(
             quantize(resid_q[h, c][0][:], resid_q[h, c][1][:], staged["resid", h, c][:])
 
         def gain_est(g, c, lo=0, hi=PACK):
-            if lo == 0:
+            if (g, c) not in work:
                 work[g, c] = keep.tile([P, PACK, WIDTH[c]], F32, name="work%d_%d" % (g, c))
             for t in range(lo, hi):
                 nc.scalar.activation(
@@ -235,6 +253,21 @@ def tile_sensing_residual_shrink_step_h3_kernel(
         def gain_wide_slots(first, count):
             for s in range(first, first + count):
                 gain_est(s // PACK, WIDE, s % PACK, s % PACK + 1)
+
+        def gain_est_on_gpsimd(slots):
+            gains = ring.tile([P, N_GROUPS, PACK], F32, name="gains", tag="gains")
+            nc.vector.tensor_copy(out=gains[:], in_=gain_bf[:])
+            for g, c, t in slots:
+                if (g, c) not in work:
+                    work[g, c] = keep.tile([P, PACK, WIDTH[c]], F32, name="work%d_%d" % (g, c))
+                nc.gpsimd.tensor_scalar(
+                    out=work[g, c][:, t, :],
+                    in0=est_raw[g, c][:, t, :],
+                    scalar1=gains[:, g, t : t + 1],
+                    scalar2=0.0,
+                    op0=ALU.mult,
+                    op1=ALU.add,
+                )
 
         def stepped(g, c):
             for t in range(PACK):
@@ -256,12 +289,16 @@ def tile_sensing_residual_shrink_step_h3_kernel(
             nc.scalar.activation(out=work[g, c][:, lo:hi, :], in_=work[g, c][:, lo:hi, :], func=ACT.Silu)
             nc.sync.dma_start(out=rows4(out_0, g)[:, lo:hi, cols(c)], in_=work[g, c][:, lo:hi, :])
 
+        def pack_y_on_scalar(g, c):
+            staged["y", g, c] = stage_s(WIDTH[c])
+            nc.scalar.copy(out=packed_view(staged["y", g, c][:]), in_=slots_view(work[g, c][:]))
+
         def pack_y(g, c):
             staged["y", g, c] = stage_v(WIDTH[c])
             nc.vector.tensor_copy(out=packed_view(staged["y", g, c][:]), in_=slots_view(work[g, c][:]))
 
         def quant_y(g, c):
-            y_codes[g, c] = ring.tile([P, WIDTH[c]], U32, name="y_codes", tag="y_codes", bufs=4, align_bytes=64)
+            y_codes[g, c] = ring.tile([P, WIDTH[c]], U32, name="y_codes%d" % c, tag="y_codes%d" % c, bufs=4, align_bytes=64)
             quantize(y_codes[g, c][:], y_scales[PACK * g :, cols(c)], staged["y", g, c][:])
 
         def store_codes(g, c):
@@ -278,28 +315,34 @@ def tile_sensing_residual_shrink_step_h3_kernel(
             if g > 0:
                 quant_turned(0, g - 1)
             quant_est(g, WIDE)
-            gain_wide_slots(3 * g, 3)
+            pack_est(g, NARROW)
+            if g == 2:
+                quant_sense(0, 0)
+            if g > 0:
+                quant_est(g - 1, NARROW)
+            pack_sense_half_on_scalar(0, g // 2, g % 2)
             turn_sense(0, g)
             if g > 0:
                 pred_pass(0, g - 1, WIDE)
             copy_turned(0, g)
-            if g == 0:
-                pack_sense(0, 0)
-        quant_sense(0, 0)
-        pack_sense(0, 1)
+            if g == 1:
+                widen_vectors()
+            if g > 0:
+                gain_est(g - 1, WIDE, 3, 4)
         quant_turned(0, last)
+        quant_est(last, NARROW)
         weigh_meas(0, WIDE)
         turn_sense(1, 0)
         pred_pass(0, last, WIDE)
         copy_turned(1, 0)
         quant_sense(0, 1)
-        pack_sense(1, 0)
+        pack_sense(0, 2)
         turn_sense(1, 1)
-        gain_wide_slots(12, 2)
         copy_turned(1, 1)
-        quant_turned(1, 0)
+        gain_est_on_gpsimd([(0, WIDE, t) for t in range(3)])
         residual(0, WIDE)
         open_acc(("pred", 1, WIDE), WIDE, 0, 1)
+        quant_turned(1, 0)
         quant_turned(1, 1)
         turn_sense(1, 2)
         copy_turned(1, 2)
@@ -308,94 +351,82 @@ def tile_sensing_residual_shrink_step_h3_kernel(
         pred_pass(1, 0, WIDE)
         pred_pass(1, 1, WIDE)
         weigh_meas(1, WIDE)
-        quant_sense(1, 0)
-        quant_turned(1, 2)
         pack_resid(0, WIDE)
+        quant_turned(1, 2)
         quant_turned(1, 3)
         pred_pass(1, 2, WIDE)
         pred_pass(1, 3, WIDE)
+        pred_narrow(0, 4)
+        pred_narrow(1, 6)
+        quant_sense(0, 2)
+        pack_sense(1, 0)
         quant_resid(0, WIDE)
-        pack_sense(1, 1)
-        gain_wide_slots(14, 2)
-        pack_est_on_scalar(0, NARROW)
-        pack_est_on_scalar(1, NARROW)
-        pack_est_on_scalar(2, NARROW)
-        residual(1, WIDE)
-        quant_sense(1, 1)
-        pack_resid(1, WIDE)
-        quant_est(0, NARROW)
-        quant_resid(1, WIDE)
-        back(0, WIDE, 0)
-        back(1, WIDE, 4)
-        quant_est(1, NARROW)
-        quant_est(2, NARROW)
-        pack_est_on_scalar(3, NARROW)
+        quant_sense(1, 0)
+        pack_sense_half_on_scalar(1, 1, 0)
+        pack_sense_half_on_scalar(1, 1, 1)
         weigh_meas(0, NARROW)
         weigh_meas(1, NARROW)
-        stepped(0, WIDE)
-        shrink(0, WIDE)
-        store_y(0, WIDE)
-        quant_est(3, NARROW)
-        pred_narrow(0, 0)
-        pred_narrow(1, 2)
-        pack_sense(0, 2)
-        stepped(1, WIDE)
-        shrink(1, WIDE)
-        quant_sense(0, 2)
-        pack_sense(1, 2)
-        quant_y(0, WIDE)
-        store_codes(0, WIDE)
-        store_y(1, WIDE)
+        pack_sense_half_on_scalar(1, 2, 0)
+        pack_sense_half_on_scalar(1, 2, 1)
+        gain_est_on_gpsimd([(1, WIDE, t) for t in range(3)])
+        residual(1, WIDE)
+        pack_resid(1, WIDE)
+        quant_sense(1, 1)
+        quant_resid(1, WIDE)
+        back(0, WIDE, 0)
         quant_sense(1, 2)
-        back(2, WIDE, 4)
+        pack_sense_half_on_scalar(0, 3, 0)
+        pack_sense_half_on_scalar(0, 3, 1)
+        gain_est_on_gpsimd([(2, WIDE, t) for t in range(3)] + [(3, WIDE, t) for t in range(4)] + [(g, NARROW, t) for g in (0, 1) for t in range(4)])
+        stepped(0, WIDE)
+        back(1, WIDE, 0)
+        shrink_slots(0, WIDE, 0, 4)
         residual(0, NARROW)
         residual(1, NARROW)
+        back(2, WIDE, 4)
+        pack_y_on_scalar(0, WIDE)
+        stepped(1, WIDE)
+        shrink_slots(1, WIDE, 0, 4)
+        stepped(2, WIDE)
+        shrink_slots(2, WIDE, 0, 4)
+        pack_sense(1, 3)
+        quant_sense(0, 3)
+        quant_sense(1, 3)
+        back(3, WIDE, 0)
         pack_resid(0, NARROW)
+        quant_y(0, WIDE)
+        store_codes(0, WIDE)
+        pack_y_on_scalar(1, WIDE)
+        gain_est_on_gpsimd([(2, NARROW, t) for t in range(4)])
+        stepped(3, WIDE)
+        pack_y_on_scalar(2, WIDE)
+        shrink_slots(3, WIDE, 0, 4)
+        pack_resid(1, NARROW)
+        quant_resid(0, NARROW)
+        quant_resid(1, NARROW)
+        back(0, NARROW, 4)
+        back(1, NARROW, 6)
+        back(2, NARROW, 0)
+        back(3, NARROW, 2)
         quant_y(1, WIDE)
         store_codes(1, WIDE)
-        gain_est(0, NARROW)
-        gain_est(1, NARROW)
-        stepped(2, WIDE)
-        shrink(2, WIDE)
-        store_y(2, WIDE)
-        quant_resid(0, NARROW)
-        pack_resid(1, NARROW)
-        pack_sense(0, 3)
-        quant_resid(1, NARROW)
-        back(0, NARROW, 0)
-        back(1, NARROW, 2)
-        quant_sense(0, 3)
-        pack_sense(1, 3)
-        stepped(0, NARROW)
-        quant_sense(1, 3)
-        back(3, WIDE, 4)
-        back(2, NARROW, 0)
-        gain_est(2, NARROW)
-        shrink(0, NARROW)
+        gain_est_on_gpsimd([(3, NARROW, t) for t in range(4)])
+        for g in range(N_GROUPS):
+            stepped(g, NARROW)
+            shrink_slots(g, NARROW, 0, 4)
         quant_y(2, WIDE)
         store_codes(2, WIDE)
-        store_y(0, NARROW)
-        stepped(1, NARROW)
-        back(3, NARROW, 2)
-        stepped(3, WIDE)
-        gain_est(3, NARROW)
-        shrink(1, NARROW)
-        quant_y(0, NARROW)
-        store_codes(0, NARROW)
-        stepped(2, NARROW)
-        quant_y(1, NARROW)
-        store_codes(1, NARROW)
-        store_y(1, NARROW)
-        shrink_slots(3, WIDE, 0, 2)
-        shrink_slots(3, WIDE, 2, 4)
-        stepped(3, NARROW)
-        shrink_slots(2, NARROW, 0, 4)
-        shrink_slots(3, NARROW, 0, 4)
         pack_y(3, WIDE)
-        pack_y(2, NARROW)
+        pack_y(0, NARROW)
         quant_y(3, WIDE)
         store_codes(3, WIDE)
-        pack_y(3, NARROW)
+        pack_y(1, NARROW)
+        quant_y(0, NARROW)
+        store_codes(0, NARROW)
+        pack_y_on_scalar(2, NARROW)
+        pack_y_on_scalar(3, NARROW)
+        quant_y(1, NARROW)
+        store_codes(1, NARROW)
         quant_y(2, NARROW)
         store_codes(2, NARROW)
         quant_y(last, NARROW)

@@ -16,421 +16,398 @@ ACT = mybir.ActivationFunctionType
 ALU = mybir.AluOpType
 
 P = 128
-PACK = 4
-GROUP = P * PACK
-M_GROUPS = M // GROUP
-N_GROUPS = N // GROUP
+SLOTS = 4
+GROUP = P * SLOTS
+MEAS_GROUPS = M // GROUP
+ATOM_GROUPS = N // GROUP
 BANK = 512
-WIDE, NARROW = 0, 1
-COL0 = (0, 512)
-WIDTH = (512, 256)
+WIDE = slice(0, 512)
+NARROW = slice(512, B)
+ALL = slice(0, B)
+LINE = 4
+STAGE_DEPTH = 3
 
 
 def tile_sensing_residual_shrink_step_h3_kernel(
     tc, sense, est, meas, weight, gain, step, out_0, out_1, out_2
 ):
     nc = tc.nc
+    last = ATOM_GROUPS - 1
     with ExitStack() as ctx:
         keep = ctx.enter_context(tc.tile_pool(name="keep", bufs=1))
-        ring = ctx.enter_context(tc.tile_pool(name="ring", bufs=2))
+        ring = ctx.enter_context(tc.tile_pool(name="ring", bufs=1))
         psum = ctx.enter_context(tc.psum_pool(name="psum", bufs=1))
         ctx.enter_context(tc.manual_schedule())
 
-        def cols(c):
-            return slice(COL0[c], COL0[c] + WIDTH[c])
+        def width(cols):
+            return cols.stop - cols.start
 
-        def rows4(dram, g):
-            return dram[g * GROUP : (g + 1) * GROUP, :].rearrange("(p t) w -> p t w", t=PACK)
+        def by_slot(dram, g):
+            return dram[g * GROUP : (g + 1) * GROUP, :].rearrange("(p t) w -> p t w", t=SLOTS)
 
         def bank(i):
             return psum.tile([P, BANK], F32, name="bank%d" % i, tag="bank%d" % i)
 
-        def operand(name, width):
-            codes = keep.tile([P, width], U32, name=name + "_codes", align_bytes=64)
-            scales = keep.tile([P, width], U8, name=name + "_scales", align_bytes=64)
-            return codes, scales
-
-        def quantize(codes, scales, staged):
-            nc.vector.quantize_mx(out=codes.bitcast(FP8X4), scales=scales, in_=staged)
-
-        def packed_view(staged):
-            return staged.rearrange("p (c i t) -> p c t i", i=4, t=PACK)
-
-        def slots_view(slots):
-            return slots.rearrange("p t (c i) -> p c t i", i=4)
-
-        def stage_v(width):
-            staged = ring.tile([P, PACK * width], BF16, name="stage_v", tag="stage_v", bufs=3, align_bytes=64)
-            return staged
-
-        def stage_s(width):
-            staged = ring.tile([P, PACK * width], BF16, name="stage_s", tag="stage_s", bufs=3, align_bytes=64)
-            return staged
-
-        gain_bf = keep.tile([P, N_GROUPS, PACK], BF16)
-        weight_bf = keep.tile([P, M_GROUPS, PACK], BF16)
-        step_bf = keep.tile([P, N_GROUPS, PACK], BF16)
         est_raw, sense_raw, meas_raw = {}, {}, {}
 
+        def load_vector(queue, name, vec, groups):
+            tile = keep.tile([P, groups, SLOTS], BF16, name=name)
+            queue.dma_start(out=tile[:], in_=vec.rearrange("(g p t) -> p g t", p=P, t=SLOTS))
+            return tile
+
         def load_est(g):
-            whole = keep.tile([P, PACK, B], BF16, name="est_raw%d" % g)
-            nc.sync.dma_start(out=whole[:], in_=rows4(est, g))
-            for c in (WIDE, NARROW):
-                est_raw[g, c] = whole[:, :, cols(c)]
+            est_raw[g] = keep.tile([P, SLOTS, B], BF16, name="est_raw%d" % g)
+            nc.sync.dma_start(out=est_raw[g][:], in_=by_slot(est, g))
 
         def load_sense(h, g):
-            sense_raw[h, g] = keep.tile([P, PACK, GROUP], BF16, name="sense_raw%d_%d" % (h, g))
-            nc.sync.dma_start(out=sense_raw[h, g][:], in_=rows4(sense, h)[:, :, g * GROUP : (g + 1) * GROUP])
+            sense_raw[h, g] = keep.tile([P, SLOTS, GROUP], BF16, name="sense_raw%d_%d" % (h, g))
+            nc.sync.dma_start(out=sense_raw[h, g][:], in_=by_slot(sense, h)[:, :, g * GROUP : (g + 1) * GROUP])
 
-        def load_meas(h, c):
-            meas_raw[h, c] = keep.tile([P, PACK, WIDTH[c]], BF16, name="meas_raw%d_%d" % (h, c))
-            nc.sync.dma_start(out=meas_raw[h, c][:], in_=rows4(meas, h)[:, :, cols(c)])
+        def load_meas(h, cols):
+            meas_raw[h, cols.start] = keep.tile([P, SLOTS, width(cols)], BF16, name="meas_raw%d_%d" % (h, cols.start))
+            nc.sync.dma_start(out=meas_raw[h, cols.start][:], in_=by_slot(meas, h)[:, :, cols])
 
-        def load_vector(tile, vec):
-            nc.sync.dma_start(out=tile[:], in_=vec.rearrange("(g p t) -> p g t", p=P, t=PACK))
-
-        for g in range(N_GROUPS):
+        gain_bf = load_vector(nc.scalar, "gain_bf", gain, ATOM_GROUPS)
+        for g in range(2):
             load_est(g)
             load_sense(0, g)
-            if g == 1:
-                load_vector(weight_bf, weight)
-                load_vector(gain_bf, gain)
-                load_vector(step_bf, step)
+        weight_bf = load_vector(nc.sync, "weight_bf", weight, MEAS_GROUPS)
+        step_bf = load_vector(nc.sync, "step_bf", step, ATOM_GROUPS)
+        for g in range(2, ATOM_GROUPS):
+            load_est(g)
+            load_sense(0, g)
         load_meas(0, WIDE)
-        for g in range(N_GROUPS):
+        for g in range(ATOM_GROUPS):
             load_sense(1, g)
         load_meas(1, WIDE)
-        for h in range(M_GROUPS):
-            load_meas(h, NARROW)
+        load_meas(0, NARROW)
+        load_meas(1, NARROW)
 
         ident = keep.tile([P, P], F32)
         make_identity(nc, ident[:])
 
-        warm = keep.tile([P, 1], F32)
-        nc.scalar.activation(out=warm[:], in_=ident[:, 0:1], func=ACT.Silu)
-        gain_f = keep.tile([P, N_GROUPS, PACK], F32)
-        weight_f = keep.tile([P, M_GROUPS, PACK], F32)
-        neg_weight_f = keep.tile([P, M_GROUPS, PACK], F32)
+        gain_f = keep.tile([P, ATOM_GROUPS, SLOTS], F32)
+        weight_f = keep.tile([P, MEAS_GROUPS, SLOTS], F32)
+        neg_weight_f = keep.tile([P, MEAS_GROUPS, SLOTS], F32)
+        nc.scalar.copy(out=gain_f[:], in_=gain_bf[:])
 
-        def widen_vectors():
-            nc.scalar.copy(out=gain_f[:], in_=gain_bf[:])
+        def widen_weight():
             nc.scalar.copy(out=weight_f[:], in_=weight_bf[:])
             nc.scalar.activation(out=neg_weight_f[:], in_=weight_bf[:], func=ACT.Copy, scale=-1.0)
 
-        staged = {}
-        est_q, sense_n_q, sense_m_q, resid_q = {}, {}, {}, {}
-        acc, turned, work, wmeas, resid, y_codes = {}, {}, {}, {}, {}, {}
-        y_scales = keep.tile([P, B], U8, align_bytes=64)
+        packed = {}
+        operand = {}
 
-        def pack_est(g, c):
-            staged["est", g, c] = stage_v(WIDTH[c])
-            nc.vector.tensor_copy(out=packed_view(staged["est", g, c][:]), in_=slots_view(est_raw[g, c][:]))
+        def stage(key, columns, tag, depth):
+            packed[key] = ring.tile([P, SLOTS * columns], BF16, name=tag, tag=tag, bufs=depth, align_bytes=64)
+            return packed[key][:]
 
-        def pack_est_on_scalar(g, c):
-            staged["est", g, c] = stage_s(WIDTH[c])
-            nc.scalar.copy(out=packed_view(staged["est", g, c][:]), in_=slots_view(est_raw[g, c][:]))
+        def pack_views(dst, src):
+            return dict(
+                out=dst.rearrange("p (c i t) -> p c t i", i=LINE, t=SLOTS),
+                in_=src.rearrange("p t (c i) -> p c t i", i=LINE),
+            )
 
-        def quant_est(g, c):
-            est_q[g, c] = operand("est%d_%d" % (g, c), WIDTH[c])
-            quantize(est_q[g, c][0][:], est_q[g, c][1][:], staged["est", g, c][:])
+        def pack_on_vector(key, src):
+            nc.vector.tensor_copy(**pack_views(stage(key, src.shape[2], "by_vector", STAGE_DEPTH), src))
+
+        def pack_on_scalar(key, src):
+            nc.scalar.copy(**pack_views(stage(key, src.shape[2], "by_scalar", STAGE_DEPTH), src))
+
+        def quantize(key):
+            columns = packed[key].shape[1] // SLOTS
+            name = "%s%d_%d" % key
+            codes = keep.tile([P, columns], U32, name=name + "_codes", align_bytes=64)
+            scales = keep.tile([P, columns], U8, name=name + "_scales", align_bytes=64)
+            nc.vector.quantize_mx(out=codes[:].bitcast(FP8X4), scales=scales[:], in_=packed[key][:])
+            operand[key] = codes, scales
+
+        def est_key(g, cols):
+            return "est", g, cols.start
+
+        def resid_key(h, cols):
+            return "resid", h, cols.start
+
+        def pack_est(g, cols):
+            pack_on_vector(est_key(g, cols), est_raw[g][:, :, cols])
+
+        turned = {}
 
         def turn_sense(h, g):
-            first = 4 + 2 * ((h * N_GROUPS + g) % 2)
+            first = 4 + 2 * (g % 2)
             turned[h, g] = [bank(first), bank(first + 1)]
-            for t in range(PACK):
+            for t in range(SLOTS):
                 words = sense_raw[h, g][:, t, :].bitcast(F32)
                 for u in range(2):
                     j = 2 * (t % 2) + u
                     nc.tensor.transpose(turned[h, g][t // 2][:, j * P : (j + 1) * P], words[:, u : 2 * P : 2], ident[:])
 
         def copy_turned(h, g):
-            staged["turn", h, g] = stage_s(GROUP)
-            dst = staged["turn", h, g][:].bitcast(F32).rearrange("p (t r u) -> p t r u", t=PACK, u=2)
+            dst = stage(("along_atoms", h, g), GROUP, "by_scalar", STAGE_DEPTH)
+            words = dst.bitcast(F32).rearrange("p (t r u) -> p t r u", t=SLOTS, u=2)
             for half in range(2):
                 src = turned[h, g][half][:].rearrange("p (t u r) -> p t r u", t=2, u=2)
-                nc.scalar.copy(out=dst[:, 2 * half : 2 * half + 2], in_=src)
+                nc.scalar.copy(out=words[:, 2 * half : 2 * half + 2], in_=src)
 
-        def quant_turned(h, g):
-            sense_n_q[h, g] = operand("sense_n%d_%d" % (h, g), GROUP)
-            quantize(sense_n_q[h, g][0][:], sense_n_q[h, g][1][:], staged["turn", h, g][:])
+        def quantize_turned(h, g):
+            quantize(("along_atoms", h, g))
 
         def sense_views(h, g):
-            dst = staged["sense", h, g][:].rearrange("p (s a i j) -> p a j i s", s=PACK, i=2, j=PACK)
-            src = sense_raw[h, g][:].rearrange("p j (a i s) -> p a j i s", i=2, s=PACK)
+            dst = packed["along_meas", h, g][:].rearrange("p (s a i t) -> p a s i t", s=SLOTS, i=2, t=SLOTS)
+            src = sense_raw[h, g][:].rearrange("p t (a i s) -> p a s i t", i=2, s=SLOTS)
             return dst, src
 
         def pack_sense(h, g):
-            staged["sense", h, g] = stage_v(GROUP)
+            stage(("along_meas", h, g), GROUP, "by_vector", STAGE_DEPTH)
             dst, src = sense_views(h, g)
             nc.vector.tensor_copy(out=dst, in_=src)
 
         def pack_sense_half_on_scalar(h, g, half):
             if half == 0:
-                staged["sense", h, g] = ring.tile([P, PACK * GROUP], BF16, name="stage_h", tag="stage_h", bufs=2, align_bytes=64)
+                stage(("along_meas", h, g), GROUP, "sense_by_scalar", 2)
             dst, src = sense_views(h, g)
-            nc.scalar.copy(out=dst[:, 32 * half : 32 * half + 32], in_=src[:, 32 * half : 32 * half + 32])
+            part = slice(half * P // 4, (half + 1) * P // 4)
+            nc.scalar.copy(out=dst[:, part], in_=src[:, part])
 
-        def quant_sense(h, g):
-            sense_m_q[h, g] = operand("sense_m%d_%d" % (h, g), GROUP)
-            quantize(sense_m_q[h, g][0][:], sense_m_q[h, g][1][:], staged["sense", h, g][:])
+        def pack_sense_on_scalar(h, g):
+            pack_sense_half_on_scalar(h, g, 0)
+            pack_sense_half_on_scalar(h, g, 1)
 
-        def open_acc(key, c, first_bank, per_bank):
-            banks = [bank(first_bank + i) for i in range(PACK // per_bank)]
-            acc[key] = [
-                banks[t // per_bank][:, (t % per_bank) * WIDTH[c] : (t % per_bank + 1) * WIDTH[c]] for t in range(PACK)
-            ]
+        def quantize_sense(h, g):
+            quantize(("along_meas", h, g))
 
         def mx_pass(out, stationary, t, moving, start, stop):
+            slot = slice(t * P, (t + 1) * P)
             nc.tensor.matmul_mx(
                 out=out,
-                lhsT=stationary[0][:, t * P : (t + 1) * P].bitcast(FP8X4),
-                lhsT_scale=stationary[1][:, t * P : (t + 1) * P],
-                rhs=moving[0][:].bitcast(FP8X4),
-                rhs_scale=moving[1][:],
+                lhsT=operand[stationary][0][:, slot].bitcast(FP8X4),
+                lhsT_scale=operand[stationary][1][:, slot],
+                rhs=operand[moving][0][:].bitcast(FP8X4),
+                rhs_scale=operand[moving][1][:],
                 start=start,
                 stop=stop,
             )
 
-        def pred_pass(h, g, c):
-            for t in range(PACK):
-                mx_pass(acc["pred", h, c][t], sense_n_q[h, g], t, est_q[g, c], g == 0, g == N_GROUPS - 1)
+        def narrow_halves(i):
+            halves = bank(i)[:].rearrange("p (t w) -> p t w", t=2)
+            return [halves[:, 0, :], halves[:, 1, :]]
 
-        def pred_narrow(h, first_bank):
-            open_acc(("pred", h, NARROW), NARROW, first_bank, 2)
-            for t in range(PACK):
-                for g in range(N_GROUPS):
-                    mx_pass(acc["pred", h, NARROW][t], sense_n_q[h, g], t, est_q[g, NARROW], g == 0, g == N_GROUPS - 1)
+        pred, back = {}, {}
 
-        def back(g, c, first_bank):
-            open_acc(("back", g, c), c, first_bank, BANK // WIDTH[c])
-            for t in range(PACK):
-                for h in range(M_GROUPS):
-                    mx_pass(acc["back", g, c][t], sense_m_q[h, g], t, resid_q[h, c], h == 0, h == M_GROUPS - 1)
+        def pred_wide_pass(h, g):
+            for t in range(SLOTS):
+                if g == 0:
+                    pred[h, WIDE.start, t] = bank(t)[:]
+                mx_pass(pred[h, WIDE.start, t], ("along_atoms", h, g), t, est_key(g, WIDE), g == 0, g == last)
 
-        def weigh_meas(h, c):
-            if c == WIDE:
-                wmeas[h, c] = ring.tile([P, PACK, WIDTH[c]], F32, name="wmeas", tag="wmeas", bufs=1)
-            elif h == 0:
-                both = ring.tile([P, M_GROUPS, PACK, WIDTH[c]], F32, name="wmeas", tag="wmeas", bufs=1)
-                wmeas[0, c], wmeas[1, c] = both[:, 0], both[:, 1]
-            for t in range(PACK):
+        def pred_narrow(h):
+            views = narrow_halves(4 + 2 * h) + narrow_halves(5 + 2 * h)
+            for t in range(SLOTS):
+                pred[h, NARROW.start, t] = views[t]
+                for g in range(ATOM_GROUPS):
+                    mx_pass(views[t], ("along_atoms", h, g), t, est_key(g, NARROW), g == 0, g == last)
+
+        def back_slot(g, cols, t, view):
+            back[g, cols.start, t] = view
+            for h in range(MEAS_GROUPS):
+                mx_pass(view, ("along_meas", h, g), t, resid_key(h, cols), h == 0, h == MEAS_GROUPS - 1)
+
+        def back_wide(g, t):
+            back_slot(g, WIDE, t, bank(t)[:])
+
+        def back_narrow(g, pair):
+            views = narrow_halves(4 + 2 * (g % 2) + pair)
+            for i in range(2):
+                back_slot(g, NARROW, 2 * pair + i, views[i])
+
+        weighted, resid = {}, {}
+
+        def weigh_meas(h, cols, dst):
+            weighted[h, cols.start] = dst
+            for t in range(SLOTS):
                 nc.scalar.activation(
-                    out=wmeas[h, c][:, t, :], in_=meas_raw[h, c][:, t, :], func=ACT.Copy, scale=weight_f[:, h, t : t + 1]
+                    out=dst[:, t, :], in_=meas_raw[h, cols.start][:, t, :], func=ACT.Copy, scale=weight_f[:, h, t : t + 1]
                 )
 
-        def residual(h, c):
-            if c == WIDE:
-                resid[h, c] = ring.tile([P, PACK, WIDTH[c]], BF16, name="resid", tag="resid", bufs=1)
-            elif h == 0:
-                both = ring.tile([P, M_GROUPS, PACK, WIDTH[c]], BF16, name="resid", tag="resid", bufs=1)
-                resid[0, c], resid[1, c] = both[:, 0], both[:, 1]
-            for t in range(PACK):
+        def residual(h, cols, dst):
+            resid[h, cols.start] = dst
+            for t in range(SLOTS):
                 nc.vector.scalar_tensor_tensor(
-                    out=resid[h, c][:, t, :],
-                    in0=acc["pred", h, c][t],
+                    out=dst[:, t, :],
+                    in0=pred[h, cols.start, t],
                     scalar=neg_weight_f[:, h, t : t + 1],
-                    in1=wmeas[h, c][:, t, :],
+                    in1=weighted[h, cols.start][:, t, :],
                     op0=ALU.mult,
                     op1=ALU.add,
                 )
 
-        def pack_resid(h, c):
-            staged["resid", h, c] = stage_v(WIDTH[c])
-            nc.vector.tensor_copy(out=packed_view(staged["resid", h, c][:]), in_=slots_view(resid[h, c][:]))
+        def wide_buffer(tag, dtype):
+            return ring.tile([P, SLOTS, width(WIDE)], dtype, name=tag, tag=tag)[:]
 
-        def quant_resid(h, c):
-            resid_q[h, c] = operand("resid%d_%d" % (h, c), WIDTH[c])
-            quantize(resid_q[h, c][0][:], resid_q[h, c][1][:], staged["resid", h, c][:])
+        def narrow_buffers(tag, dtype):
+            return ring.tile([P, MEAS_GROUPS, SLOTS, width(NARROW)], dtype, name=tag, tag=tag)
 
-        def gain_est(g, c, lo=0, hi=PACK):
-            if (g, c) not in work:
-                work[g, c] = keep.tile([P, PACK, WIDTH[c]], F32, name="work%d_%d" % (g, c))
-            for t in range(lo, hi):
+        result = [keep.tile([P, SLOTS, B], F32, name="result%d" % g) for g in range(ATOM_GROUPS)]
+        y_codes = [keep.tile([P, B], U32, name="y_codes%d" % g, align_bytes=64) for g in range(ATOM_GROUPS)]
+        y_scales = keep.tile([P, B], U8, align_bytes=64)
+
+        def gain_est_on_scalar(g, cols, slots):
+            for t in slots:
                 nc.scalar.activation(
-                    out=work[g, c][:, t, :], in_=est_raw[g, c][:, t, :], func=ACT.Copy, scale=gain_f[:, g, t : t + 1]
+                    out=result[g][:, t, cols], in_=est_raw[g][:, t, cols], func=ACT.Copy, scale=gain_f[:, g, t : t + 1]
                 )
 
-        def gain_wide_slots(first, count):
-            for s in range(first, first + count):
-                gain_est(s // PACK, WIDE, s % PACK, s % PACK + 1)
-
-        def gain_est_on_gpsimd(slots):
-            gains = ring.tile([P, N_GROUPS, PACK], F32, name="gains", tag="gains")
+        def gain_est_on_gpsimd(groups, cols, slots):
+            gains = ring.tile([P, ATOM_GROUPS, SLOTS], F32, name="gains", tag="gains")
             nc.vector.tensor_copy(out=gains[:], in_=gain_bf[:])
-            for g, c, t in slots:
-                if (g, c) not in work:
-                    work[g, c] = keep.tile([P, PACK, WIDTH[c]], F32, name="work%d_%d" % (g, c))
-                nc.gpsimd.tensor_scalar(
-                    out=work[g, c][:, t, :],
-                    in0=est_raw[g, c][:, t, :],
-                    scalar1=gains[:, g, t : t + 1],
-                    scalar2=0.0,
-                    op0=ALU.mult,
-                    op1=ALU.add,
-                )
+            for g in groups:
+                for t in slots:
+                    nc.gpsimd.tensor_scalar(
+                        out=result[g][:, t, cols],
+                        in0=est_raw[g][:, t, cols],
+                        scalar1=gains[:, g, t : t + 1],
+                        scalar2=0.0,
+                        op0=ALU.mult,
+                        op1=ALU.add,
+                    )
 
-        def stepped(g, c):
-            for t in range(PACK):
-                nc.vector.scalar_tensor_tensor(
-                    out=work[g, c][:, t, :],
-                    in0=acc["back", g, c][t],
-                    scalar=step_bf[:, g, t : t + 1],
-                    in1=work[g, c][:, t, :],
-                    op0=ALU.mult,
-                    op1=ALU.add,
-                )
+        def add_step(g, cols, t):
+            nc.vector.scalar_tensor_tensor(
+                out=result[g][:, t, cols],
+                in0=back[g, cols.start, t],
+                scalar=step_bf[:, g, t : t + 1],
+                in1=result[g][:, t, cols],
+                op0=ALU.mult,
+                op1=ALU.add,
+            )
 
-        def shrink(g, c):
-            staged["y", g, c] = stage_s(WIDTH[c])
-            nc.scalar.activation(out=packed_view(staged["y", g, c][:]), in_=slots_view(work[g, c][:]), func=ACT.Silu)
-            nc.scalar.activation(out=work[g, c][:], in_=work[g, c][:], func=ACT.Silu)
+        def shrink_and_store(g, pair):
+            slots = slice(2 * pair, 2 * pair + 2)
+            nc.scalar.activation(out=result[g][:, slots, :], in_=result[g][:, slots, :], func=ACT.Silu)
+            nc.sync.dma_start(out=by_slot(out_0, g)[:, slots, :], in_=result[g][:, slots, :])
 
-        def shrink_slots(g, c, lo, hi):
-            nc.scalar.activation(out=work[g, c][:, lo:hi, :], in_=work[g, c][:, lo:hi, :], func=ACT.Silu)
-            nc.sync.dma_start(out=rows4(out_0, g)[:, lo:hi, cols(c)], in_=work[g, c][:, lo:hi, :])
+        def y_key(g, cols):
+            return "y", g, cols.start
 
-        def pack_y_on_scalar(g, c):
-            staged["y", g, c] = stage_s(WIDTH[c])
-            nc.scalar.copy(out=packed_view(staged["y", g, c][:]), in_=slots_view(work[g, c][:]))
+        def quantize_y(g, cols):
+            nc.vector.quantize_mx(
+                out=y_codes[g][:, cols].bitcast(FP8X4),
+                scales=y_scales[SLOTS * g :, cols],
+                in_=packed[y_key(g, cols)][:],
+            )
 
-        def pack_y(g, c):
-            staged["y", g, c] = stage_v(WIDTH[c])
-            nc.vector.tensor_copy(out=packed_view(staged["y", g, c][:]), in_=slots_view(work[g, c][:]))
-
-        def quant_y(g, c):
-            y_codes[g, c] = ring.tile([P, WIDTH[c]], U32, name="y_codes%d" % c, tag="y_codes%d" % c, bufs=4, align_bytes=64)
-            quantize(y_codes[g, c][:], y_scales[PACK * g :, cols(c)], staged["y", g, c][:])
-
-        def store_codes(g, c):
+        def finish_planes(g):
             words = out_1[g].rearrange("p m t -> p (m t)").bitcast(I32)
-            nc.sync.dma_start(out=words[:, cols(c)], in_=y_codes[g, c][:].bitcast(I32))
+            for cols in (WIDE, NARROW):
+                quantize_y(g, cols)
+                nc.sync.dma_start(out=words[:, cols], in_=y_codes[g][:, cols].bitcast(I32))
 
-        def store_y(g, c):
-            nc.sync.dma_start(out=rows4(out_0, g)[:, :, cols(c)], in_=work[g, c][:])
 
-        last = N_GROUPS - 1
-        open_acc(("pred", 0, WIDE), WIDE, 0, 1)
-        for g in range(N_GROUPS):
+        for g in range(ATOM_GROUPS):
             pack_est(g, WIDE)
             if g > 0:
-                quant_turned(0, g - 1)
-            quant_est(g, WIDE)
+                quantize_turned(0, g - 1)
+            else:
+                gain_est_on_scalar(0, WIDE, range(2))
             pack_est(g, NARROW)
-            if g == 2:
-                quant_sense(0, 0)
+            quantize(est_key(g, WIDE))
             if g > 0:
-                quant_est(g - 1, NARROW)
+                quantize(est_key(g - 1, NARROW))
             pack_sense_half_on_scalar(0, g // 2, g % 2)
             turn_sense(0, g)
             if g > 0:
-                pred_pass(0, g - 1, WIDE)
+                pred_wide_pass(0, g - 1)
             copy_turned(0, g)
-            if g == 1:
-                widen_vectors()
-            if g > 0:
-                gain_est(g - 1, WIDE, 3, 4)
-        quant_turned(0, last)
-        quant_est(last, NARROW)
-        weigh_meas(0, WIDE)
+            if g in (1, 2):
+                gain_est_on_scalar(0, WIDE, [g + 1])
+            if g == 2:
+                quantize_sense(0, 0)
+        widen_weight()
+        weigh_meas(0, WIDE, wide_buffer("weighted", F32))
+        quantize_turned(0, last)
+        quantize(est_key(last, NARROW))
+
         turn_sense(1, 0)
-        pred_pass(0, last, WIDE)
+        pred_wide_pass(0, last)
         copy_turned(1, 0)
-        quant_sense(0, 1)
-        pack_sense(0, 2)
-        turn_sense(1, 1)
-        copy_turned(1, 1)
-        gain_est_on_gpsimd([(0, WIDE, t) for t in range(3)])
-        residual(0, WIDE)
-        open_acc(("pred", 1, WIDE), WIDE, 0, 1)
-        quant_turned(1, 0)
-        quant_turned(1, 1)
-        turn_sense(1, 2)
-        copy_turned(1, 2)
-        turn_sense(1, 3)
-        copy_turned(1, 3)
-        pred_pass(1, 0, WIDE)
-        pred_pass(1, 1, WIDE)
-        weigh_meas(1, WIDE)
-        pack_resid(0, WIDE)
-        quant_turned(1, 2)
-        quant_turned(1, 3)
-        pred_pass(1, 2, WIDE)
-        pred_pass(1, 3, WIDE)
-        pred_narrow(0, 4)
-        pred_narrow(1, 6)
-        quant_sense(0, 2)
         pack_sense(1, 0)
-        quant_resid(0, WIDE)
-        quant_sense(1, 0)
-        pack_sense_half_on_scalar(1, 1, 0)
-        pack_sense_half_on_scalar(1, 1, 1)
-        weigh_meas(0, NARROW)
-        weigh_meas(1, NARROW)
-        pack_sense_half_on_scalar(1, 2, 0)
-        pack_sense_half_on_scalar(1, 2, 1)
-        gain_est_on_gpsimd([(1, WIDE, t) for t in range(3)])
-        residual(1, WIDE)
-        pack_resid(1, WIDE)
-        quant_sense(1, 1)
-        quant_resid(1, WIDE)
-        back(0, WIDE, 0)
-        quant_sense(1, 2)
-        pack_sense_half_on_scalar(0, 3, 0)
-        pack_sense_half_on_scalar(0, 3, 1)
-        gain_est_on_gpsimd([(2, WIDE, t) for t in range(3)] + [(3, WIDE, t) for t in range(4)] + [(g, NARROW, t) for g in (0, 1) for t in range(4)])
-        stepped(0, WIDE)
-        back(1, WIDE, 0)
-        shrink_slots(0, WIDE, 0, 4)
-        residual(0, NARROW)
-        residual(1, NARROW)
-        back(2, WIDE, 4)
-        pack_y_on_scalar(0, WIDE)
-        stepped(1, WIDE)
-        shrink_slots(1, WIDE, 0, 4)
-        stepped(2, WIDE)
-        shrink_slots(2, WIDE, 0, 4)
+        quantize_sense(0, 1)
+        turn_sense(1, 1)
+        pack_sense_half_on_scalar(0, 2, 0)
+        copy_turned(1, 1)
+        gain_est_on_gpsimd([1], WIDE, range(2))
+        residual(0, WIDE, wide_buffer("resid", BF16))
+        quantize_turned(1, 0)
+        quantize_turned(1, 1)
+        for g in range(2, ATOM_GROUPS):
+            turn_sense(1, g)
+            copy_turned(1, g)
+        weigh_meas(1, WIDE, wide_buffer("weighted", F32))
+        pack_on_vector(resid_key(0, WIDE), resid[0, WIDE.start])
+        quantize_turned(1, 2)
+        quantize_turned(1, 3)
+        for g in range(ATOM_GROUPS):
+            pred_wide_pass(1, g)
+        for h in range(MEAS_GROUPS):
+            pred_narrow(h)
+
+        pack_sense_half_on_scalar(0, 2, 1)
+        pack_sense_on_scalar(1, 1)
+        quantize_sense(1, 0)
         pack_sense(1, 3)
-        quant_sense(0, 3)
-        quant_sense(1, 3)
-        back(3, WIDE, 0)
-        pack_resid(0, NARROW)
-        quant_y(0, WIDE)
-        store_codes(0, WIDE)
-        pack_y_on_scalar(1, WIDE)
-        gain_est_on_gpsimd([(2, NARROW, t) for t in range(4)])
-        stepped(3, WIDE)
-        pack_y_on_scalar(2, WIDE)
-        shrink_slots(3, WIDE, 0, 4)
-        pack_resid(1, NARROW)
-        quant_resid(0, NARROW)
-        quant_resid(1, NARROW)
-        back(0, NARROW, 4)
-        back(1, NARROW, 6)
-        back(2, NARROW, 0)
-        back(3, NARROW, 2)
-        quant_y(1, WIDE)
-        store_codes(1, WIDE)
-        gain_est_on_gpsimd([(3, NARROW, t) for t in range(4)])
-        for g in range(N_GROUPS):
-            stepped(g, NARROW)
-            shrink_slots(g, NARROW, 0, 4)
-        quant_y(2, WIDE)
-        store_codes(2, WIDE)
-        pack_y(3, WIDE)
-        pack_y(0, NARROW)
-        quant_y(3, WIDE)
-        store_codes(3, WIDE)
-        pack_y(1, NARROW)
-        quant_y(0, NARROW)
-        store_codes(0, NARROW)
-        pack_y_on_scalar(2, NARROW)
-        pack_y_on_scalar(3, NARROW)
-        quant_y(1, NARROW)
-        store_codes(1, NARROW)
-        quant_y(2, NARROW)
-        store_codes(2, NARROW)
-        quant_y(last, NARROW)
-        store_codes(last, NARROW)
+        quantize(resid_key(0, WIDE))
+        quantize_sense(0, 2)
+        quantize_sense(1, 3)
+        gain_est_on_gpsimd([1], WIDE, range(2, SLOTS))
+        residual(1, WIDE, wide_buffer("resid", BF16))
+        pack_sense_half_on_scalar(1, 2, 0)
+        narrow_weighted = narrow_buffers("weighted", F32)
+        for h in range(MEAS_GROUPS):
+            weigh_meas(h, NARROW, narrow_weighted[:, h])
+        pack_sense_half_on_scalar(1, 2, 1)
+        pack_on_vector(resid_key(1, WIDE), resid[1, WIDE.start])
+        quantize_sense(1, 1)
+        quantize(resid_key(1, WIDE))
+        pack_sense_on_scalar(0, 3)
+        for t in range(SLOTS):
+            back_wide(0, t)
+        narrow_resid = narrow_buffers("resid", BF16)
+        for h in range(MEAS_GROUPS):
+            residual(h, NARROW, narrow_resid[:, h])
+        gain_est_on_scalar(0, NARROW, range(SLOTS))
+        for h in range(MEAS_GROUPS):
+            pack_on_vector(resid_key(h, NARROW), resid[h, NARROW.start])
+        gain_est_on_scalar(1, NARROW, range(SLOTS))
+        for h in range(MEAS_GROUPS):
+            quantize(resid_key(h, NARROW))
+        for pair in range(2):
+            back_narrow(0, pair)
+        quantize_sense(1, 2)
+        quantize_sense(0, 3)
+
+        gain_est_on_gpsimd([2, 3], ALL, range(SLOTS))
+        for g in range(ATOM_GROUPS):
+            for pair in range(2):
+                if g < last:
+                    back_narrow(g + 1, pair)
+                for t in (2 * pair, 2 * pair + 1):
+                    add_step(g, WIDE, t)
+                    if g < last:
+                        back_wide(g + 1, t)
+                    add_step(g, NARROW, t)
+                shrink_and_store(g, pair)
+
+        for g in range(ATOM_GROUPS):
+            if g < last:
+                pack_on_vector(y_key(g, WIDE), result[g][:, :, WIDE])
+            else:
+                pack_on_scalar(y_key(g, WIDE), result[g][:, :, WIDE])
+            if g == 0:
+                pack_on_vector(y_key(g, NARROW), result[g][:, :, NARROW])
+            else:
+                pack_on_scalar(y_key(g, NARROW), result[g][:, :, NARROW])
+                finish_planes(g - 1)
+        finish_planes(last)
         scale_rows = out_2.bitcast(I32)
         for q in range(4):
             nc.scalar.dma_start(

@@ -89,6 +89,7 @@ def tile_sensing_residual_shrink_step_h3_kernel(
         gain_f = keep.tile([P, ATOM_GROUPS, SLOTS], F32)
         weight_f = keep.tile([P, MEAS_GROUPS, SLOTS], F32)
         neg_weight_f = keep.tile([P, MEAS_GROUPS, SLOTS], F32)
+        nc.scalar.activation(out=gain_f[:, 0, 0:1], in_=ident[:, 0:1], func=ACT.Silu)
         nc.scalar.copy(out=gain_f[:], in_=gain_bf[:])
 
         def widen_weight():
@@ -142,12 +143,16 @@ def tile_sensing_residual_shrink_step_h3_kernel(
                     j = 2 * (t % 2) + u
                     nc.tensor.transpose(turned[h, g][t // 2][:, j * P : (j + 1) * P], words[:, u : 2 * P : 2], ident[:])
 
+        def copy_turned_bank(h, g, pair):
+            if pair == 0:
+                stage(("along_atoms", h, g), GROUP, "by_scalar", STAGE_DEPTH)
+            words = packed["along_atoms", h, g][:].bitcast(F32).rearrange("p (t r u) -> p t r u", t=SLOTS, u=2)
+            src = turned[h, g][pair][:].rearrange("p (t u r) -> p t r u", t=2, u=2)
+            nc.scalar.copy(out=words[:, 2 * pair : 2 * pair + 2], in_=src)
+
         def copy_turned(h, g):
-            dst = stage(("along_atoms", h, g), GROUP, "by_scalar", STAGE_DEPTH)
-            words = dst.bitcast(F32).rearrange("p (t r u) -> p t r u", t=SLOTS, u=2)
-            for half in range(2):
-                src = turned[h, g][half][:].rearrange("p (t u r) -> p t r u", t=2, u=2)
-                nc.scalar.copy(out=words[:, 2 * half : 2 * half + 2], in_=src)
+            copy_turned_bank(h, g, 0)
+            copy_turned_bank(h, g, 1)
 
         def quantize_turned(h, g):
             quantize(("along_atoms", h, g))
@@ -257,19 +262,18 @@ def tile_sensing_residual_shrink_step_h3_kernel(
                     out=result[g][:, t, cols], in_=est_raw[g][:, t, cols], func=ACT.Copy, scale=gain_f[:, g, t : t + 1]
                 )
 
-        def gain_est_on_gpsimd(groups, cols, slots):
+        def gain_est_on_gpsimd(pieces):
             gains = ring.tile([P, ATOM_GROUPS, SLOTS], F32, name="gains", tag="gains")
             nc.vector.tensor_copy(out=gains[:], in_=gain_bf[:])
-            for g in groups:
-                for t in slots:
-                    nc.gpsimd.tensor_scalar(
-                        out=result[g][:, t, cols],
-                        in0=est_raw[g][:, t, cols],
-                        scalar1=gains[:, g, t : t + 1],
-                        scalar2=0.0,
-                        op0=ALU.mult,
-                        op1=ALU.add,
-                    )
+            for g, t, cols in pieces:
+                nc.gpsimd.tensor_scalar(
+                    out=result[g][:, t, cols],
+                    in0=est_raw[g][:, t, cols],
+                    scalar1=gains[:, g, t : t + 1],
+                    scalar2=0.0,
+                    op0=ALU.mult,
+                    op1=ALU.add,
+                )
 
         def add_step(g, cols, t):
             nc.vector.scalar_tensor_tensor(
@@ -281,10 +285,9 @@ def tile_sensing_residual_shrink_step_h3_kernel(
                 op1=ALU.add,
             )
 
-        def shrink_and_store(g, pair):
-            slots = slice(2 * pair, 2 * pair + 2)
-            nc.scalar.activation(out=result[g][:, slots, :], in_=result[g][:, slots, :], func=ACT.Silu)
-            nc.sync.dma_start(out=by_slot(out_0, g)[:, slots, :], in_=result[g][:, slots, :])
+        def shrink_and_store(g, cols, slots):
+            nc.scalar.activation(out=result[g][:, slots, cols], in_=result[g][:, slots, cols], func=ACT.Silu)
+            nc.sync.dma_start(out=by_slot(out_0, g)[:, slots, cols], in_=result[g][:, slots, cols])
 
         def y_key(g, cols):
             return "y", g, cols.start
@@ -314,10 +317,15 @@ def tile_sensing_residual_shrink_step_h3_kernel(
             if g > 0:
                 quantize(est_key(g - 1, NARROW))
             pack_sense_half_on_scalar(0, g // 2, g % 2)
+            if g == 2:
+                gain_est_on_scalar(1, NARROW, range(2))
             turn_sense(0, g)
             if g > 0:
                 pred_wide_pass(0, g - 1)
-            copy_turned(0, g)
+            copy_turned_bank(0, g, 0)
+            if g < 2:
+                gain_est_on_scalar(0, NARROW, (2 * g, 2 * g + 1))
+            copy_turned_bank(0, g, 1)
             if g in (1, 2):
                 gain_est_on_scalar(0, WIDE, [g + 1])
             if g == 2:
@@ -335,7 +343,7 @@ def tile_sensing_residual_shrink_step_h3_kernel(
         turn_sense(1, 1)
         pack_sense_half_on_scalar(0, 2, 0)
         copy_turned(1, 1)
-        gain_est_on_gpsimd([1], WIDE, range(2))
+        gain_est_on_gpsimd([(1, 0, WIDE), (1, 1, WIDE)])
         residual(0, WIDE, wide_buffer("resid", BF16))
         quantize_turned(1, 0)
         quantize_turned(1, 1)
@@ -358,7 +366,7 @@ def tile_sensing_residual_shrink_step_h3_kernel(
         quantize(resid_key(0, WIDE))
         quantize_sense(0, 2)
         quantize_sense(1, 3)
-        gain_est_on_gpsimd([1], WIDE, range(2, SLOTS))
+        gain_est_on_gpsimd([(1, 2, WIDE), (1, 3, WIDE)])
         residual(1, WIDE, wide_buffer("resid", BF16))
         pack_sense_half_on_scalar(1, 2, 0)
         narrow_weighted = narrow_buffers("weighted", F32)
@@ -368,25 +376,33 @@ def tile_sensing_residual_shrink_step_h3_kernel(
         pack_on_vector(resid_key(1, WIDE), resid[1, WIDE.start])
         quantize_sense(1, 1)
         quantize(resid_key(1, WIDE))
-        pack_sense_on_scalar(0, 3)
         for t in range(SLOTS):
             back_wide(0, t)
+        pack_sense_on_scalar(0, 3)
+        gain_est_on_gpsimd([(1, 2, NARROW), (1, 3, NARROW), (2, 0, ALL), (2, 1, ALL)])
         narrow_resid = narrow_buffers("resid", BF16)
         for h in range(MEAS_GROUPS):
             residual(h, NARROW, narrow_resid[:, h])
-        gain_est_on_scalar(0, NARROW, range(SLOTS))
-        for h in range(MEAS_GROUPS):
-            pack_on_vector(resid_key(h, NARROW), resid[h, NARROW.start])
-        gain_est_on_scalar(1, NARROW, range(SLOTS))
+
+        for t in range(SLOTS):
+            add_step(0, WIDE, t)
+            back_wide(1, t)
+        pack_on_scalar(resid_key(0, NARROW), resid[0, NARROW.start])
+        shrink_and_store(0, WIDE, slice(0, SLOTS))
+        pack_on_scalar(y_key(0, WIDE), result[0][:, :, WIDE])
+        pack_on_vector(resid_key(1, NARROW), resid[1, NARROW.start])
         for h in range(MEAS_GROUPS):
             quantize(resid_key(h, NARROW))
-        for pair in range(2):
-            back_narrow(0, pair)
+        for g in range(2):
+            for pair in range(2):
+                back_narrow(g, pair)
         quantize_sense(1, 2)
         quantize_sense(0, 3)
-
-        gain_est_on_gpsimd([2, 3], ALL, range(SLOTS))
-        for g in range(ATOM_GROUPS):
+        gain_est_on_gpsimd([(2, 2, ALL), (2, 3, ALL)] + [(last, t, ALL) for t in range(SLOTS)])
+        for t in range(SLOTS):
+            add_step(0, NARROW, t)
+        shrink_and_store(0, NARROW, slice(0, SLOTS))
+        for g in range(1, ATOM_GROUPS):
             for pair in range(2):
                 if g < last:
                     back_narrow(g + 1, pair)
@@ -395,21 +411,22 @@ def tile_sensing_residual_shrink_step_h3_kernel(
                     if g < last:
                         back_wide(g + 1, t)
                     add_step(g, NARROW, t)
-                shrink_and_store(g, pair)
+                shrink_and_store(g, ALL, slice(2 * pair, 2 * pair + 2))
 
-        for g in range(ATOM_GROUPS):
-            if g < last:
-                pack_on_vector(y_key(g, WIDE), result[g][:, :, WIDE])
-            else:
-                pack_on_scalar(y_key(g, WIDE), result[g][:, :, WIDE])
-            if g == 0:
-                pack_on_vector(y_key(g, NARROW), result[g][:, :, NARROW])
-            else:
-                pack_on_scalar(y_key(g, NARROW), result[g][:, :, NARROW])
-                finish_planes(g - 1)
-        finish_planes(last)
+        pack_on_scalar(y_key(last - 1, NARROW), result[last - 1][:, :, NARROW])
+        pack_on_scalar(y_key(last, WIDE), result[last][:, :, WIDE])
+        pack_on_vector(y_key(0, NARROW), result[0][:, :, NARROW])
+        pack_on_vector(y_key(1, WIDE), result[1][:, :, WIDE])
+        finish_planes(0)
+        pack_on_scalar(y_key(last, NARROW), result[last][:, :, NARROW])
+        pack_on_vector(y_key(1, NARROW), result[1][:, :, NARROW])
+        pack_on_vector(y_key(2, WIDE), result[2][:, :, WIDE])
+        for g in range(1, ATOM_GROUPS):
+            finish_planes(g)
         scale_rows = out_2.bitcast(I32)
-        for q in range(4):
-            nc.scalar.dma_start(
-                out=scale_rows[:, 4 * q : 4 * q + 4, :], in_=y_scales[32 * q : 32 * q + 16, :].bitcast(I32)
+        for quadrant in range(4):
+            queue = nc.scalar if quadrant < 2 else nc.sync
+            queue.dma_start(
+                out=scale_rows[:, 4 * quadrant : 4 * quadrant + 4, :],
+                in_=y_scales[32 * quadrant : 32 * quadrant + 16, :].bitcast(I32),
             )

from contextlib import ExitStack

import concourse.mybir as mybir
from concourse.masks import make_identity

M, N, B = 1024, 2048, 768
FLOPS = 2 * 2 * M * N * B

F32 = mybir.dt.float32
BF16 = mybir.dt.bfloat16
U32 = mybir.dt.uint32
I32 = mybir.dt.int32
U8 = mybir.dt.uint8
FP8X4 = mybir.dt.float8_e4m3fn_x4
ACT = mybir.ActivationFunctionType
ALU = mybir.AluOpType

P = 128
SLOTS = 4
GROUP = P * SLOTS
MEAS_GROUPS = M // GROUP
ATOM_GROUPS = N // GROUP
BANK = 512
WIDE = slice(0, 512)
NARROW = slice(512, B)
ALL = slice(0, B)
LINE = 4
STAGE_DEPTH = 3


def tile_sensing_residual_shrink_step_h3_kernel(
    tc, sense, est, meas, weight, gain, step, out_0, out_1, out_2
):
    nc = tc.nc
    last = ATOM_GROUPS - 1
    with ExitStack() as ctx:
        keep = ctx.enter_context(tc.tile_pool(name="keep", bufs=1))
        ring = ctx.enter_context(tc.tile_pool(name="ring", bufs=1))
        psum = ctx.enter_context(tc.psum_pool(name="psum", bufs=1))
        ctx.enter_context(tc.manual_schedule())

        def width(cols):
            return cols.stop - cols.start

        def by_slot(dram, g):
            return dram[g * GROUP : (g + 1) * GROUP, :].rearrange("(p t) w -> p t w", t=SLOTS)

        def bank(i):
            return psum.tile([P, BANK], F32, name="bank%d" % i, tag="bank%d" % i)

        est_raw, sense_raw, meas_raw = {}, {}, {}

        def load_vector(queue, name, vec, groups):
            tile = keep.tile([P, groups, SLOTS], BF16, name=name)
            queue.dma_start(out=tile[:], in_=vec.rearrange("(g p t) -> p g t", p=P, t=SLOTS))
            return tile

        def load_est(g):
            est_raw[g] = keep.tile([P, SLOTS, B], BF16, name="est_raw%d" % g)
            nc.sync.dma_start(out=est_raw[g][:], in_=by_slot(est, g))

        def load_sense(h, g):
            sense_raw[h, g] = keep.tile([P, SLOTS, GROUP], BF16, name="sense_raw%d_%d" % (h, g))
            nc.sync.dma_start(out=sense_raw[h, g][:], in_=by_slot(sense, h)[:, :, g * GROUP : (g + 1) * GROUP])

        def load_meas(h, cols):
            meas_raw[h, cols.start] = keep.tile([P, SLOTS, width(cols)], BF16, name="meas_raw%d_%d" % (h, cols.start))
            nc.sync.dma_start(out=meas_raw[h, cols.start][:], in_=by_slot(meas, h)[:, :, cols])

        gain_bf = load_vector(nc.scalar, "gain_bf", gain, ATOM_GROUPS)
        for g in range(2):
            load_est(g)
            load_sense(0, g)
        weight_bf = load_vector(nc.sync, "weight_bf", weight, MEAS_GROUPS)
        step_bf = load_vector(nc.sync, "step_bf", step, ATOM_GROUPS)
        for g in range(2, ATOM_GROUPS):
            load_est(g)
            load_sense(0, g)
        load_meas(0, WIDE)
        for g in range(ATOM_GROUPS):
            load_sense(1, g)
        load_meas(1, WIDE)
        load_meas(0, NARROW)
        load_meas(1, NARROW)

        ident = keep.tile([P, P], F32)
        make_identity(nc, ident[:])

        gain_f = keep.tile([P, ATOM_GROUPS, SLOTS], F32)
        weight_f = keep.tile([P, MEAS_GROUPS, SLOTS], F32)
        neg_weight_f = keep.tile([P, MEAS_GROUPS, SLOTS], F32)
        nc.scalar.activation(out=gain_f[:, 0, 0:1], in_=ident[:, 0:1], func=ACT.Silu)
        nc.scalar.copy(out=gain_f[:], in_=gain_bf[:])

        def widen_weight():
            nc.scalar.copy(out=weight_f[:], in_=weight_bf[:])
            nc.scalar.activation(out=neg_weight_f[:], in_=weight_bf[:], func=ACT.Copy, scale=-1.0)

        packed = {}
        operand = {}

        def stage(key, columns, tag, depth):
            packed[key] = ring.tile([P, SLOTS * columns], BF16, name=tag, tag=tag, bufs=depth, align_bytes=64)
            return packed[key][:]

        def pack_views(dst, src):
            return dict(
                out=dst.rearrange("p (c i t) -> p c t i", i=LINE, t=SLOTS),
                in_=src.rearrange("p t (c i) -> p c t i", i=LINE),
            )

        def pack_on_vector(key, src):
            nc.vector.tensor_copy(**pack_views(stage(key, src.shape[2], "by_vector", STAGE_DEPTH), src))

        def pack_on_scalar(key, src):
            nc.scalar.copy(**pack_views(stage(key, src.shape[2], "by_scalar", STAGE_DEPTH), src))

        def quantize(key):
            columns = packed[key].shape[1] // SLOTS
            name = "%s%d_%d" % key
            codes = keep.tile([P, columns], U32, name=name + "_codes", align_bytes=64)
            scales = keep.tile([P, columns], U8, name=name + "_scales", align_bytes=64)
            nc.vector.quantize_mx(out=codes[:].bitcast(FP8X4), scales=scales[:], in_=packed[key][:])
            operand[key] = codes, scales

        def est_key(g, cols):
            return "est", g, cols.start

        def resid_key(h, cols):
            return "resid", h, cols.start

        def pack_est(g, cols):
            pack_on_vector(est_key(g, cols), est_raw[g][:, :, cols])

        turned = {}

        def turn_sense(h, g):
            first = 4 + 2 * (g % 2)
            turned[h, g] = [bank(first), bank(first + 1)]
            for t in range(SLOTS):
                words = sense_raw[h, g][:, t, :].bitcast(F32)
                for u in range(2):
                    j = 2 * (t % 2) + u
                    nc.tensor.transpose(turned[h, g][t // 2][:, j * P : (j + 1) * P], words[:, u : 2 * P : 2], ident[:])

        def copy_turned_bank(h, g, pair):
            if pair == 0:
                stage(("along_atoms", h, g), GROUP, "by_scalar", STAGE_DEPTH)
            words = packed["along_atoms", h, g][:].bitcast(F32).rearrange("p (t r u) -> p t r u", t=SLOTS, u=2)
            src = turned[h, g][pair][:].rearrange("p (t u r) -> p t r u", t=2, u=2)
            nc.scalar.copy(out=words[:, 2 * pair : 2 * pair + 2], in_=src)

        def copy_turned(h, g):
            copy_turned_bank(h, g, 0)
            copy_turned_bank(h, g, 1)

        def quantize_turned(h, g):
            quantize(("along_atoms", h, g))

        def sense_views(h, g):
            dst = packed["along_meas", h, g][:].rearrange("p (s a i t) -> p a s i t", s=SLOTS, i=2, t=SLOTS)
            src = sense_raw[h, g][:].rearrange("p t (a i s) -> p a s i t", i=2, s=SLOTS)
            return dst, src

        def pack_sense(h, g):
            stage(("along_meas", h, g), GROUP, "by_vector", STAGE_DEPTH)
            dst, src = sense_views(h, g)
            nc.vector.tensor_copy(out=dst, in_=src)

        def pack_sense_half_on_scalar(h, g, half):
            if half == 0:
                stage(("along_meas", h, g), GROUP, "sense_by_scalar", 2)
            dst, src = sense_views(h, g)
            part = slice(half * P // 4, (half + 1) * P // 4)
            nc.scalar.copy(out=dst[:, part], in_=src[:, part])

        def pack_sense_on_scalar(h, g):
            pack_sense_half_on_scalar(h, g, 0)
            pack_sense_half_on_scalar(h, g, 1)

        def quantize_sense(h, g):
            quantize(("along_meas", h, g))

        def mx_pass(out, stationary, t, moving, start, stop):
            slot = slice(t * P, (t + 1) * P)
            nc.tensor.matmul_mx(
                out=out,
                lhsT=operand[stationary][0][:, slot].bitcast(FP8X4),
                lhsT_scale=operand[stationary][1][:, slot],
                rhs=operand[moving][0][:].bitcast(FP8X4),
                rhs_scale=operand[moving][1][:],
                start=start,
                stop=stop,
            )

        def narrow_halves(i):
            halves = bank(i)[:].rearrange("p (t w) -> p t w", t=2)
            return [halves[:, 0, :], halves[:, 1, :]]

        pred, back = {}, {}

        def pred_wide_pass(h, g):
            for t in range(SLOTS):
                if g == 0:
                    pred[h, WIDE.start, t] = bank(t)[:]
                mx_pass(pred[h, WIDE.start, t], ("along_atoms", h, g), t, est_key(g, WIDE), g == 0, g == last)

        def pred_narrow(h):
            views = narrow_halves(4 + 2 * h) + narrow_halves(5 + 2 * h)
            for t in range(SLOTS):
                pred[h, NARROW.start, t] = views[t]
                for g in range(ATOM_GROUPS):
                    mx_pass(views[t], ("along_atoms", h, g), t, est_key(g, NARROW), g == 0, g == last)

        def back_slot(g, cols, t, view):
            back[g, cols.start, t] = view
            for h in range(MEAS_GROUPS):
                mx_pass(view, ("along_meas", h, g), t, resid_key(h, cols), h == 0, h == MEAS_GROUPS - 1)

        def back_wide(g, t):
            back_slot(g, WIDE, t, bank(t)[:])

        def back_narrow(g, pair):
            views = narrow_halves(4 + 2 * (g % 2) + pair)
            for i in range(2):
                back_slot(g, NARROW, 2 * pair + i, views[i])

        weighted, resid = {}, {}

        def weigh_meas(h, cols, dst):
            weighted[h, cols.start] = dst
            for t in range(SLOTS):
                nc.scalar.activation(
                    out=dst[:, t, :], in_=meas_raw[h, cols.start][:, t, :], func=ACT.Copy, scale=weight_f[:, h, t : t + 1]
                )

        def residual(h, cols, dst):
            resid[h, cols.start] = dst
            for t in range(SLOTS):
                nc.vector.scalar_tensor_tensor(
                    out=dst[:, t, :],
                    in0=pred[h, cols.start, t],
                    scalar=neg_weight_f[:, h, t : t + 1],
                    in1=weighted[h, cols.start][:, t, :],
                    op0=ALU.mult,
                    op1=ALU.add,
                )

        def wide_buffer(tag, dtype):
            return ring.tile([P, SLOTS, width(WIDE)], dtype, name=tag, tag=tag)[:]

        def narrow_buffers(tag, dtype):
            return ring.tile([P, MEAS_GROUPS, SLOTS, width(NARROW)], dtype, name=tag, tag=tag)

        result = [keep.tile([P, SLOTS, B], F32, name="result%d" % g) for g in range(ATOM_GROUPS)]
        y_codes = [keep.tile([P, B], U32, name="y_codes%d" % g, align_bytes=64) for g in range(ATOM_GROUPS)]
        y_scales = keep.tile([P, B], U8, align_bytes=64)

        def gain_est_on_scalar(g, cols, slots):
            for t in slots:
                nc.scalar.activation(
                    out=result[g][:, t, cols], in_=est_raw[g][:, t, cols], func=ACT.Copy, scale=gain_f[:, g, t : t + 1]
                )

        def gain_est_on_gpsimd(pieces):
            gains = ring.tile([P, ATOM_GROUPS, SLOTS], F32, name="gains", tag="gains")
            nc.vector.tensor_copy(out=gains[:], in_=gain_bf[:])
            for g, t, cols in pieces:
                nc.gpsimd.tensor_scalar(
                    out=result[g][:, t, cols],
                    in0=est_raw[g][:, t, cols],
                    scalar1=gains[:, g, t : t + 1],
                    scalar2=0.0,
                    op0=ALU.mult,
                    op1=ALU.add,
                )

        def add_step(g, cols, t):
            nc.vector.scalar_tensor_tensor(
                out=result[g][:, t, cols],
                in0=back[g, cols.start, t],
                scalar=step_bf[:, g, t : t + 1],
                in1=result[g][:, t, cols],
                op0=ALU.mult,
                op1=ALU.add,
            )

        def shrink_and_store(g, cols, slots):
            nc.scalar.activation(out=result[g][:, slots, cols], in_=result[g][:, slots, cols], func=ACT.Silu)
            nc.sync.dma_start(out=by_slot(out_0, g)[:, slots, cols], in_=result[g][:, slots, cols])

        def y_key(g, cols):
            return "y", g, cols.start

        def quantize_y(g, cols):
            nc.vector.quantize_mx(
                out=y_codes[g][:, cols].bitcast(FP8X4),
                scales=y_scales[SLOTS * g :, cols],
                in_=packed[y_key(g, cols)][:],
            )

        def finish_planes(g):
            words = out_1[g].rearrange("p m t -> p (m t)").bitcast(I32)
            for cols in (WIDE, NARROW):
                quantize_y(g, cols)
                nc.sync.dma_start(out=words[:, cols], in_=y_codes[g][:, cols].bitcast(I32))


        for g in range(ATOM_GROUPS):
            pack_est(g, WIDE)
            if g > 0:
                quantize_turned(0, g - 1)
            else:
                gain_est_on_scalar(0, WIDE, range(2))
            pack_est(g, NARROW)
            quantize(est_key(g, WIDE))
            if g > 0:
                quantize(est_key(g - 1, NARROW))
            pack_sense_half_on_scalar(0, g // 2, g % 2)
            if g == 2:
                gain_est_on_scalar(1, NARROW, range(2))
            turn_sense(0, g)
            if g > 0:
                pred_wide_pass(0, g - 1)
            copy_turned_bank(0, g, 0)
            if g < 2:
                gain_est_on_scalar(0, NARROW, (2 * g, 2 * g + 1))
            copy_turned_bank(0, g, 1)
            if g in (1, 2):
                gain_est_on_scalar(0, WIDE, [g + 1])
            if g == 2:
                quantize_sense(0, 0)
        widen_weight()
        weigh_meas(0, WIDE, wide_buffer("weighted", F32))
        quantize_turned(0, last)
        quantize(est_key(last, NARROW))

        turn_sense(1, 0)
        pred_wide_pass(0, last)
        copy_turned(1, 0)
        pack_sense(1, 0)
        quantize_sense(0, 1)
        turn_sense(1, 1)
        pack_sense_half_on_scalar(0, 2, 0)
        copy_turned(1, 1)
        gain_est_on_gpsimd([(1, 0, WIDE), (1, 1, WIDE)])
        residual(0, WIDE, wide_buffer("resid", BF16))
        quantize_turned(1, 0)
        quantize_turned(1, 1)
        for g in range(2, ATOM_GROUPS):
            turn_sense(1, g)
            copy_turned(1, g)
        weigh_meas(1, WIDE, wide_buffer("weighted", F32))
        pack_on_vector(resid_key(0, WIDE), resid[0, WIDE.start])
        quantize_turned(1, 2)
        quantize_turned(1, 3)
        for g in range(ATOM_GROUPS):
            pred_wide_pass(1, g)
        for h in range(MEAS_GROUPS):
            pred_narrow(h)

        pack_sense_half_on_scalar(0, 2, 1)
        pack_sense_on_scalar(1, 1)
        quantize_sense(1, 0)
        pack_sense(1, 3)
        quantize(resid_key(0, WIDE))
        quantize_sense(0, 2)
        quantize_sense(1, 3)
        gain_est_on_gpsimd([(1, 2, WIDE), (1, 3, WIDE)])
        residual(1, WIDE, wide_buffer("resid", BF16))
        pack_sense_half_on_scalar(1, 2, 0)
        narrow_weighted = narrow_buffers("weighted", F32)
        for h in range(MEAS_GROUPS):
            weigh_meas(h, NARROW, narrow_weighted[:, h])
        pack_sense_half_on_scalar(1, 2, 1)
        pack_on_vector(resid_key(1, WIDE), resid[1, WIDE.start])
        quantize_sense(1, 1)
        quantize(resid_key(1, WIDE))
        for t in range(SLOTS):
            back_wide(0, t)
        pack_sense_on_scalar(0, 3)
        gain_est_on_gpsimd([(1, 2, NARROW), (1, 3, NARROW), (2, 0, ALL), (2, 1, ALL)])
        narrow_resid = narrow_buffers("resid", BF16)
        for h in range(MEAS_GROUPS):
            residual(h, NARROW, narrow_resid[:, h])

        for t in range(SLOTS):
            add_step(0, WIDE, t)
            back_wide(1, t)
        pack_on_scalar(resid_key(0, NARROW), resid[0, NARROW.start])
        shrink_and_store(0, WIDE, slice(0, SLOTS))
        pack_on_scalar(y_key(0, WIDE), result[0][:, :, WIDE])
        pack_on_vector(resid_key(1, NARROW), resid[1, NARROW.start])
        for h in range(MEAS_GROUPS):
            quantize(resid_key(h, NARROW))
        for g in range(2):
            for pair in range(2):
                back_narrow(g, pair)
        quantize_sense(1, 2)
        quantize_sense(0, 3)
        gain_est_on_gpsimd([(2, 2, ALL), (2, 3, ALL)] + [(last, t, ALL) for t in range(SLOTS)])
        for t in range(SLOTS):
            add_step(0, NARROW, t)
        shrink_and_store(0, NARROW, slice(0, SLOTS))
        for g in range(1, ATOM_GROUPS):
            for pair in range(2):
                if g < last:
                    back_narrow(g + 1, pair)
                for t in (2 * pair, 2 * pair + 1):
                    add_step(g, WIDE, t)
                    if g < last:
                        back_wide(g + 1, t)
                    add_step(g, NARROW, t)
                shrink_and_store(g, ALL, slice(2 * pair, 2 * pair + 2))

        pack_on_scalar(y_key(last - 1, NARROW), result[last - 1][:, :, NARROW])
        pack_on_scalar(y_key(last, WIDE), result[last][:, :, WIDE])
        pack_on_vector(y_key(0, NARROW), result[0][:, :, NARROW])
        pack_on_vector(y_key(1, WIDE), result[1][:, :, WIDE])
        finish_planes(0)
        pack_on_scalar(y_key(last, NARROW), result[last][:, :, NARROW])
        pack_on_vector(y_key(1, NARROW), result[1][:, :, NARROW])
        pack_on_vector(y_key(2, WIDE), result[2][:, :, WIDE])
        for g in range(1, ATOM_GROUPS):
            finish_planes(g)
        scale_rows = out_2.bitcast(I32)
        for quadrant in range(4):
            queue = nc.scalar if quadrant < 2 else nc.sync
            queue.dma_start(
                out=scale_rows[:, 4 * quadrant : 4 * quadrant + 4, :],
                in_=y_scales[32 * quadrant : 32 * quadrant + 16, :].bitcast(I32),
            )
